import numpy as np, ml_dtypes
CORES = [2,3,42,43,82,83,122,123]
N = 8
import mx_ref
BF = ml_dtypes.bfloat16
def gentries(a):
    return np.ascontiguousarray(a.reshape(8, 16, -1).transpose(0, 2, 1)).reshape(8, -1)
def gtable(e):
    e = np.asarray(e); return np.ascontiguousarray(e.reshape(8, -1, 16).transpose(0, 2, 1)).reshape(128, -1).astype(np.int32)
def gpick(z, e):
    return np.concatenate([z[16 * g:16 * g + 16][:, e[g]] for g in range(8)])
def cols(t, e):
    v = np.concatenate([t.reshape(128, -1, 4), np.zeros((128, 1, 4), BF)], axis=1)
    return np.ascontiguousarray(v[:, e]).reshape(128, -1)
def pick(q, e):
    c = np.concatenate([q[0].reshape(128, -1, 4), np.zeros((128, 1, 4), np.uint8)], axis=1); s = np.concatenate([q[1], np.ones((16, 1), np.uint8)], axis=1)
    return (np.ascontiguousarray(c[:, e].reshape(128, -1)), np.ascontiguousarray(s[:, e]))
def join(*qs):
    return (np.concatenate([q[0] for q in qs], axis=1), np.concatenate([q[1] for q in qs], axis=1))
def put(q, e, v):
    c, s = q[0].reshape(128, -1, 4).copy(), q[1].copy(); c[:, e] = v[0].reshape(128, -1, 4); s[:, e] = v[1]
    return (c.reshape(128, -1), s)
def pk(c, s):
    return (np.ascontiguousarray(c), mx_ref.live(s))
def emit(q):
    return q[0], q[1]
def values_of_codes():
    e, c = np.zeros((128, 128, 4), np.float32), np.zeros((128, 2, 4), np.uint8)
    e[np.arange(128), np.arange(128), 0] = 1
    c[:127, :, 0] = np.arange(256).reshape(2, 128).T[:127]
    return mx_ref.matmul(mx_ref.quantize(e.reshape(128, 512).astype(BF)), (c.reshape(128, 8), np.full((16, 2), 127, np.uint8))).T.reshape(-1).astype(np.float64)
CODE_VALUE, SCALE_VALUE = values_of_codes(), 2.0 ** (np.arange(256) - 127.0)
def decode(q):
    return (CODE_VALUE[q[0]].reshape(16, 8, -1, 4) * SCALE_VALUE[q[1]][:, None, :, None] + 0.0).reshape(128, -1).astype(np.float32)
def f(rng, *shape):
    return mx_ref.flush((rng.standard_normal(shape, dtype=np.float32) * np.exp2(rng.integers(-2, 3, shape[:-1] + (1,)))).astype(BF))
def wide(rng, *shape, cols=0):
    v = rng.standard_normal(shape, dtype=np.float32) * np.exp2(rng.integers(-12, 13, shape)).astype(np.float32)
    if cols: v *= np.repeat(np.exp2(rng.integers(-cols, cols + 1, shape[:-2] + (1, shape[-1] // 4))) * (rng.random(shape[:-2] + (1, shape[-1] // 4)) > 0.0625), 4, axis=-1).astype(np.float32)
    return mx_ref.flush(v.astype(BF))
T, S, CAPP, R = 4, 448, 16, 2
def coarse(v):
    v = v.astype(np.float32)
    v[np.abs(v) < np.float32(2.0 ** -16)] = 0
    return v.astype(BF)
def numbers_of(rng):
    return {"x": coarse(f(rng, N, 128, 512 * T)), "e": coarse(f(rng, N, 128, 4 * S)), "v": np.array(f(rng, N, 128, 512))}
def lists_of(rng):
    return {k: np.stack([gtable(rng.integers(0, S, (8, S))) for r in range(N)]) for k in ("pa", "pb")}
def signs(rng):
    return np.stack([rng.permutation(128) % 2 * 2.0 - 1.0 for r in range(N)]).astype(np.float32)
def setup_inputs(rng):
    return {**numbers_of(rng), **lists_of(rng)}
def setup_inputs_ties(rng):
    d = setup_inputs(rng)
    x = d["x"].reshape(N, 128, T, 128, 4)
    x[:, :, :, ::8] = 0
    for r in range(N):
        run = np.concatenate([rng.permutation(4), rng.permutation(4)])
        k = run[np.arange(S) * 8 // S]
        d["e"][r] = cols(d["e"][r], np.where(k == 3, -1, k))
        same = np.argsort(k, kind="stable").reshape(4, S // 4)
        a, b = gentries(d["pa"][r]), gentries(d["pb"][r])
        d["pb"][r] = gtable(np.where(rng.random((8, S)) < 0.5, same[k[a], rng.integers(0, S // 4, (8, S))], b))
    return {**d, "x": x.reshape(N, 128, 512 * T)}
def setup_inputs_near(rng):
    d = setup_inputs(rng)
    x = d["x"].reshape(N, 128, T, 128, 4)
    x[:, :96] = 0
    x[:, 0, :, :, 0] = signs(rng)[:, None, :].astype(BF)
    x[:, 8:10] = (rng.choice([-1.0, 1.0], (N, 2, T, 128, 4)) * 2.0 ** -4).astype(np.float32).astype(BF)
    e = d["e"].reshape(N, 128, S, 4)
    m = np.zeros((N, 128), bool)
    for r in range(N): m[r, 32 + 8 * r:40 + 8 * r] = True
    e[~m] = 0
    e[:, 0, :, 0] = 1
    s = np.arange(S) // 2
    g = (((s[:, None] >> np.arange(8)) & 1) * np.exp2(np.arange(8) - 19.0)).astype(np.float32).astype(BF)
    e[:, 8] = g[:, :4]
    e[:, 9] = g[:, 4:]
    for r in range(N):
        d["pb"][r] = gtable(gentries(d["pa"][r]) ^ rng.choice(np.array([1, 2, 2, 4]), (8, S)))
    small = np.float32(2.0 ** -8)
    return {**d, "x": (x.astype(np.float32) * small).astype(BF).reshape(N, 128, 512 * T), "e": (e.astype(np.float32) * small).astype(BF).reshape(N, 128, 4 * S)}
def setup_inputs_huge(rng):
    d = setup_inputs(rng)
    g = (rng.permutation(N) % 2 * 2.0 - 1.0) * 2.0 ** 26
    x = rng.integers(12, 16, (N, 128, T, 128, 4)) * 2.0 ** 26 * signs(rng)[:, None, None, :, None]
    e = rng.permuted(np.tile(np.arange(512) % 4 + 12, (N, S, 1)), axis=2).reshape(N, S, 128, 4).transpose(0, 2, 1, 3) * g[:, None, None, None]
    d["x"] = x.astype(np.float32).reshape(N, 128, 512 * T).astype(BF)
    d["e"] = np.ascontiguousarray(e.astype(np.float32)).reshape(N, 128, 4 * S).astype(BF)
    return d
def setup_inputs_crowd(rng):
    d = setup_inputs(rng)
    x = d["x"].reshape(N, 128, T, 128, 4)
    e = d["e"].reshape(N, 128, S, 4)
    x[:, 0:8 * N:8] = 0
    e[:, 0:8 * N:8] = 0
    e[:, np.arange(S) // (S // N) * 8, np.arange(S), 0] = 1024
    o = rng.permutation(N)
    rest = np.array([c for c in o if c not in (o[0], o[1], o[3])])
    for r in range(N):
        to = np.full(128, o[1])
        if r != o[0] and r != o[1]:
            to[:CAPP] = o[0]
            to[2 * CAPP + 1:] = np.resize(rest, 128 - 2 * CAPP - 1)
        to = rng.permutation(to)
        x[r, 8 * to, T - 1, np.arange(128), 0] = 4096
    return {**d, "x": x.reshape(N, 128, 512 * T), "e": e.reshape(N, 128, 4 * S)}
def setup_inputs_spread(rng):
    d = setup_inputs(rng)
    d["x"] = coarse(wide(rng, N, 128, 512 * T, cols=6))
    d["e"] = coarse(wide(rng, N, 128, 4 * S))
    return d
def check_inputs(d):
    b = []
    for k in ("x", "e", "v"):
        a = np.abs(d[k].astype(np.float32))
        if not (np.isfinite(a).all() and ((a == 0) | (a >= 2.0 ** -30) & (a <= 2.0 ** 30)).all()): b.append("a value of " + k)
    for k in ("pa", "pb"):
        if not ((d[k] >= 0) & (d[k] < S)).all(): b.append("an entry of " + k)
    return b
def trace(q, w, a, b):
    p = np.arange(128)
    s = mx_ref.matmul(pick(q, p), w)
    came = []
    for t in range(1, T):
        m, n = gpick(s, a), gpick(s, b)
        came.append(np.where(n > m, np.repeat(b, 16, axis=0), np.repeat(a, 16, axis=0)))
        s = np.maximum(m, n) + mx_ref.matmul(pick(q, 128 * t + p), w)
    path = np.zeros((128, T), int)
    path[:, T - 1] = np.argmax(s + np.float32(0.0), axis=1)
    for t in range(T - 1, 0, -1): path[:, t - 1] = came[t - 1][p, path[:, t]]
    return path
def reference(x, e, v, pa, pb):
    a, b = [gentries(pa[r]) for r in range(N)], [gentries(pb[r]) for r in range(N)]
    qe = [mx_ref.quantize(e[r]) for r in range(N)]
    data = join(*[mx_ref.quantize(x[r]) for r in range(N)])
    mine = [128 * T * r + np.arange(128 * T) for r in range(N)]
    for turn in range(R):
        home = [trace(pick(data, mine[r]), qe[r], a[r], b[r]) for r in range(N)]
        visit, at, new = [], [], []
        for c in range(N):
            slot = np.full((T, 128), -1)
            for r in range(N):
                p = np.flatnonzero(home[r][:, T - 1] // (S // N) == c)[:CAPP]
                slot[:, CAPP * r:CAPP * r + len(p)] = 128 * T * r + 128 * np.arange(T)[:, None] + p
            slot = slot.reshape(-1)
            q = pick(data, slot)
            path = trace(q, qe[c], a[c], b[c])
            z = (decode(q) + decode(pick(qe[c], path.transpose().reshape(-1)))) * np.float32(0.5)
            full = np.flatnonzero(slot >= 0)
            at.append(slot[full])
            new.append(pick(mx_ref.quantize(np.ascontiguousarray(z.astype(BF))), full))
            visit.append(path)
        data = put(data, np.concatenate(at), join(*new))
    y, ol, dl = np.zeros((N, 128, 128 * T), np.float32), np.zeros((N, 128, T), np.float32), np.zeros((N, N * CAPP, T), np.float32)
    oc, osc = np.zeros((N, 128, 512 * T), np.uint8), np.zeros((N, 16, 128 * T), np.uint8)
    for r in range(N):
        q = pick(data, mine[r])
        y[r] = mx_ref.matmul(mx_ref.quantize(v[r]), q)
        ol[r] = home[r]
        dl[r] = visit[r][:N * CAPP]
        oc[r], osc[r] = emit(q)
    return {"y": y, "ol": ol, "dl": dl, "oc": oc, "osc": osc}

@@ -1,0 +1,526 @@
+from concourse.bass import DstId, RemoteDMATransfer
+from concourse.mybir import dt, AluOpType, ActivationFunctionType
+
+ALU = AluOpType
+ACT = ActivationFunctionType
+N, TT, S, CAP = 8, 4, 448, 16
+W = 144
+HW = TT * W
+PC = TT * CAP
+NH = 2
+CUT = 160
+C4, U8 = "float8_e4m3fn_x4", "uint8"
+
+SCRATCH = {
+    "xin": ("sbuf", [128, 4 * HW], "bfloat16"), "ein": ("sbuf", [128, 4 * S], "bfloat16"), "vin": ("sbuf", [128, 512], "bfloat16"),
+    "pai": ("sbuf", [128, 28], "int32"), "pbi": ("sbuf", [128, 28], "int32"),
+    "pau": ("sbuf", [128, 28], "uint16"), "pbu": ("sbuf", [128, 28], "uint16"),
+    "et": ("sbuf", [128, 2048], "bfloat16"), "nt1": ("sbuf", [128, 2048], "bfloat16"), "nt2": ("sbuf", [128, 2048], "bfloat16"),
+    "aa": ("sbuf", [128, TT * S], "float32"), "bt": ("sbuf", [128, 8 * S], "float32"), "rr": ("sbuf", [128, S], "float32"),
+    "junk": ("sbuf", [128, S], "float32"), "ysb": ("sbuf", [128, 512], "float32"),
+    "pci": ("sbuf", [128, 1], "int32"), "pcf": ("sbuf", [128, 1], "float32"), "bitsi": ("sbuf", [128, 2], "int32"),
+    "bits": ("sbuf", [128, 4], "float32"), "jm16": ("sbuf", [128, 128], "float32"), "mask": ("sbuf", [128, 128], "float32"),
+    "rst": ("sbuf", [128, 128], "float32"), "kmin": ("sbuf", [128, 128], "float32"), "cap": ("sbuf", [128, 128], "bfloat16"),
+    "i448": ("sbuf", [128, S], "float32"), "trow": ("sbuf", [128, 4], "float32"), "xa": ("sbuf", [128, 4], "float32"),
+    "ft": ("sbuf", [128, 32], "float32"), "ft2": ("sbuf", [128, 32], "float32"), "ft3": ("sbuf", [128, 32], "float32"),
+    "fl": ("sbuf", [128, 2], "uint16"), "gz": ("sbuf", [128, 512], "float32"), "mi": ("sbuf", [128, 128], "float32"),
+    "tr": ("sbuf", [128, 128], "float32"), "dcol": ("sbuf", [128, 2], "float32"), "db": ("sbuf", [128, 32], "bfloat16"),
+    "row": ("sbuf", [128, 128], "bfloat16"), "eq": ("sbuf", [128, 128], "bfloat16"), "cum": ("sbuf", [128, 128], "bfloat16"),
+    "offs": ("sbuf", [128, 128], "uint16"), "t16": ("sbuf", [128, 4], "float32"), "xl": ("sbuf", [128, 32], "uint16"),
+    "cb": ("sbuf", [128, 12], "float32"), "tli": ("sbuf", [128, 8], "int32"), "tl": ("sbuf", [128, 8], "uint16"),
+    "j16": ("sbuf", [128, 8], "float32"), "j128": ("sbuf", [128, 8], "float32"), "valrow": ("sbuf", [128, 128], "float32"),
+    "inv": ("sbuf", [128, 256], "float32"), "w8": ("sbuf", [128, 64], "float32"), "ro": ("sbuf", [128, 8], "uint16"),
+    "rl": ("sbuf", [128, 80], "float32"), "rlu": ("sbuf", [128, 80], "uint16"),
+    "bo": ("sbuf", [128, 12], "uint16"), "gg": ("sbuf", [128, 64], "float32"), "sc": ("sbuf", [128, 64], "float32"),
+    "dd": ("sbuf", [128, 4], "float32"), "path": ("sbuf", [128, 24], "float32"),
+}
+for _n, _w in (("qe", S), ("qv", 128), ("qk", 512), ("held1", HW), ("held2", HW), ("win1", HW + 512), ("win2", HW + 512),
+               ("out1", 512), ("out2", 512), ("land1", 512), ("land2", 512), ("xs1", 512), ("xs2", 512), ("ep1", 512), ("ep2", 512),
+               ("new1", 512), ("new2", 512), ("fin", 512),
+               ("rel1", PC * max(NH, 1)), ("rel2", PC * max(NH, 1)), ("rel3", PC * max(NH, 1)), ("rel4", PC * max(NH, 1))):
+    SCRATCH[_n + "c"] = ("sbuf", [128, _w], C4)
+    SCRATCH[_n + "s"] = ("sbuf", [128, _w], U8)
+for _b in range(8):
+    SCRATCH["ps%d" % _b] = ("psum", [128, 512], "float32")
+
+SEMAPHORES = (["cv", "ca", "cp", "cg", "sent"] + ["%s%d" % (a, k) for a in ("arrc", "arrs", "relc", "rels") for k in range(1, 5)]
+              + ["d%d" % k for k in range(40)])
+
+STAGES = {1: ("out1", "land1", 0), 2: ("new1", "win1", HW), 3: ("out2", "land2", 0), 4: ("new2", "win2", HW)}
+
+
+def bits_of(engs):
+    m = 0
+    for e in engs:
+        m |= 1 << e
+    return m
+
+
+def deal(n, engs, flip):
+    sizes = [1] * n
+    while True:
+        k = sizes.index(min(sizes))
+        if sum(sizes) + sizes[k] > len(engs):
+            break
+        sizes[k] *= 2
+    if flip:
+        sizes = sizes[::-1]
+    out, at = [], 0
+    for s in sizes:
+        out.append(engs[at:at + s])
+        at += s
+    return out
+
+
+def routes(cores, topo):
+    plan = []
+    for r, c in enumerate(cores):
+        here = [k for k in range(N) if topo.chip(cores[k]) == topo.chip(c)]
+        sib = [k for k in here if k != r]
+        off = [k for k in range(N) if k not in here]
+
+        def place(k):
+            return [j for j in range(N) if topo.chip(cores[j]) == topo.chip(cores[k])].index(k)
+        like = [k for k in off if place(k) == place(r)]
+        like = ([k for k in like if not topo.same_plane(topo.chip(c), topo.chip(cores[k]))]
+                + [k for k in like if topo.same_plane(topo.chip(c), topo.chip(cores[k]))])
+        via = like[:NH]
+        direct = [k for k in off if k not in via]
+        cands = [k for k in topo.cores_of(c) if k not in cores and topo.die(k) != topo.die(c)
+                 and all(topo.may_write(k, cores[d]) for d in via)]
+        helper = cands[place(r)]
+        out_engs = topo.engines(c, cores[direct[0]])
+        in_engs = [e for e in topo.engines(c, cores[sib[0]]) if e not in out_engs]
+        eng = {}
+        for f in (0, 1):
+            for d, m in zip(direct, deal(len(direct), out_engs, f)):
+                eng[d, f] = m
+            for d, m in zip(sib, deal(len(sib), in_engs, f)):
+                eng[d, f] = m
+            if via:
+                for d, m in zip(via, deal(len(via), topo.engines(helper, cores[via[0]]), f)):
+                    eng[d, f] = m
+        plan.append({"order": via + direct + sib + [r], "via": via, "self": direct + sib, "helper": helper, "eng": eng,
+                     "heng": (topo.engines(c, helper), in_engs)})
+    return plan
+
+
+def side(T, name, f, a, b):
+    return T[name + "s"][:, a:b] if f else T[name + "c"][:, a:b].bitcast(dt.uint8)
+
+
+def pieces(g, T, topo, plan, r, dests, src, at, k, f):
+    _, land, base = STAGES[k]
+    trs, n = [], 0
+    for j, d in enumerate(dests):
+        rid, pid, _ = topo.addr(T.cores[d])
+        c = base + PC * plan[d]["order"].index(r)
+        e = plan[r]["eng"][d, f]
+        trs.append(RemoteDMATransfer(dst_ids=[DstId(rid=rid, pnc=pid)], dma_engine_mask=bits_of(e),
+                                     remote_sem=T.sem[("arrs%d" if f else "arrc%d") % k],
+                                     src=side(T, src, f, at + PC * j, at + PC * (j + 1)), dst=side(T, land, f, c, c + PC)))
+        n += len(e)
+    g.remote_dma_fused(trs, local_sem=T.sem.sent)
+    return n
+
+
+def helper_program(g, T, topo, plan, r):
+    n = 0
+    for k in range(1, 5):
+        for f in (0, 1):
+            g.wait_ge(T.sem[("rels%d" if f else "relc%d") % k], len(plan[r]["heng"][f]))
+            n += pieces(g, T, topo, plan, r, plan[r]["via"], "rel%d" % k, 0, k, f)
+    g.wait_ge(T.sem.sent, n)
+
+
+def rank_program(g, core, T, topo):
+    plan = routes(list(T.cores), topo)
+    r = T.rank_of(core)
+    if r is None:
+        for k in range(N):
+            if plan[k]["via"] and plan[k]["helper"] == core:
+                helper_program(g, T, topo, plan, k)
+        return
+    me = plan[r]
+    order = me["order"]
+    Q = {"v": g.vector, "a": g.scalar, "p": g.tensor, "s": g.sync, "g": g}
+    known = {e: {} for e in Q}
+    count, waited, hist = {}, {}, {}
+    seq, free = [0], ["d%d" % k for k in range(40)]
+
+    def v(name, a=0, b=None, step=1, p0=0, p1=128):
+        if b is None:
+            b = SCRATCH[name][1][1]
+        m = 0
+        if step == 1:
+            m = ((1 << (b - a)) - 1) << a
+        else:
+            for c in range(a, b, step):
+                m |= 1 << c
+        cs = slice(a, b) if step == 1 else slice(a, b, step)
+        ap = T[name][:, cs] if (p0, p1) == (0, 128) else T[name][p0:p1, cs]
+        return {"ap": ap, "n": name, "p": (p0, p1), "m": m}
+
+    def wait(e, sem, n, clock):
+        if known[e].get(sem, 0) >= n:
+            return
+        Q[e].wait_ge(T.sem[sem], n)
+        waited[sem] = max(waited.get(sem, 0), n)
+        known[e][sem] = n
+        for s, c in clock.items():
+            if known[e].get(s, 0) < c:
+                known[e][s] = c
+
+    def before(e, reads, writes):
+        deps = {}
+        for views, wr in ((reads, False), (writes, True)):
+            for x in views:
+                for (op, w, p, m) in hist.get(x["n"], []):
+                    if x["n"].startswith("ps"):
+                        hit = op["e"] != e
+                    else:
+                        hit = (w or wr) and p[0] < x["p"][1] and x["p"][0] < p[1] and (m & x["m"])
+                    if hit:
+                        deps[op["k"]] = op
+        for k in sorted(deps, reverse=True):
+            wait(e, deps[k]["sem"], deps[k]["n"], deps[k]["clock"])
+
+    def note(e, sem, n, reads, writes, clock):
+        seq[0] += 1
+        op = {"e": e, "sem": sem, "n": n, "k": seq[0], "clock": clock}
+        for views, wr in ((reads, False), (writes, True)):
+            for x in views:
+                hist.setdefault(x["n"], []).append((op, wr, x["p"], x["m"]))
+
+    def do(e, call, reads, writes):
+        before(e, reads, writes)
+        sem = "c" + e
+        count[sem] = count.get(sem, 0) + 1
+        call().then_inc(T.sem[sem], 1)
+        note(e, sem, count[sem], reads, writes, dict(known[e]))
+
+    def dma(e, out, in_, reads, writes):
+        before(e, reads, writes)
+        sem = free.pop(0)
+        count[sem] = 16
+        Q[e].dma_start(out, in_).then_inc(T.sem[sem], 16)
+        note("d", sem, 16, reads, writes, dict(known[e]))
+
+    def sc(x):
+        return x["ap"] if isinstance(x, dict) else x
+
+    def cols(*xs):
+        return [x for x in xs if isinstance(x, dict)]
+
+    def src(x, off):
+        return x["ap"] if off is None else x["ap"].indirect(off["ap"])
+
+    def ts(out, in0, s1, s2, op0, op1=None):
+        if op1 is None:
+            do("v", lambda: g.vector.tensor_scalar(out["ap"], in0["ap"], sc(s1), None, op0), cols(in0, s1), [out])
+        else:
+            do("v", lambda: g.vector.tensor_scalar(out["ap"], in0["ap"], sc(s1), sc(s2), op0, op1), cols(in0, s1, s2), [out])
+
+    def tt(out, in0, in1, op, off=None):
+        do("v", lambda: g.vector.tensor_tensor(out["ap"], src(in0, off), in1["ap"], op), cols(in0, in1, off), [out])
+
+    def cp(out, in_, off=None):
+        do("v", lambda: g.vector.tensor_copy(out["ap"], src(in_, off)), cols(in_, off), [out])
+
+    def scan(out, d0, d1, init, op0, op1):
+        do("v", lambda: g.vector.tensor_tensor_scan(out["ap"], d0["ap"], d1["ap"], init, op0, op1), [d0, d1], [out])
+
+    def transpose(out, in_):
+        do("v", lambda: g.vector.transpose(out["ap"], in_["ap"]), [in_], [out])
+
+    def memset(out, c):
+        do("v", lambda: g.vector.memset(out["ap"], c), [], [out])
+
+    def acopy(out, in_, off=None):
+        do("a", lambda: g.scalar.activation(out["ap"], src(in_, off), ACT.Copy), cols(in_, off), [out])
+
+    def below(acc, in_, top, n):
+        j = v("junk", 0, n)
+        do("a", lambda: g.scalar.activation(j["ap"], in_["ap"], ACT.Sign, bias=top["ap"], scale=-1.0, accum_out=acc["ap"]),
+           [in_, top], [j, acc])
+
+    def iota(out, pattern, base, cm=0, whole=False):
+        if whole:
+            do("g", lambda: g.iota(out["ap"], pattern, base, cm), [], [out])
+        else:
+            do("g", lambda: g.iota(out["ap"], pattern, base, cm, allow_small_or_imprecise_dtypes=True), [], [out])
+
+    def quant(name, a, b, tile, ta):
+        c, s, t = v(name + "c", a, b), v(name + "s", a, b), v(tile, 4 * ta, 4 * (ta + b - a))
+        do("v", lambda: g.vector.quantize_mx(c["ap"], s["ap"], t["ap"]), [t], [c, s])
+
+    def pickc(dst, a, b, win, n, off):
+        o, w = v(dst + "c", a, b), v(win + "c", 0, n)
+        do("v", lambda: g.vector.tensor_copy(o["ap"].bitcast(dt.uint32), w["ap"].bitcast(dt.uint32).indirect(off["ap"])), [w, off], [o])
+
+    def picks(dst, a, b, win, n, off):
+        acopy(v(dst + "s", a, b), v(win + "s", 0, n), off)
+
+    def pick(dst, a, b, win, n, off):
+        pickc(dst, a, b, win, n, off)
+        picks(dst, a, b, win, n, off)
+
+    def mm(bank, w, wa, x, xa, n, start=True, stop=True):
+        o = v("ps%d" % bank, 0, n)
+        wc, ws, xc, xs = v(w + "c", wa, wa + 128), v(w + "s", wa, wa + 128), v(x + "c", xa, xa + n), v(x + "s", xa, xa + n)
+        do("p", lambda: g.tensor.matmul_mx(o["ap"], wc["ap"], ws["ap"], xc["ap"], xs["ap"], start, stop), [wc, ws, xc, xs], [o])
+
+    def move(e, dst, a, b, from_, fa):
+        for f in (0, 1):
+            x = "s" if f else "c"
+            dma(e, side(T, dst, f, a, b), side(T, from_, f, fa, fa + b - a), [v(from_ + x, fa, fa + b - a)], [v(dst + x, a, b)])
+
+    sent = [0]
+
+    def to_helper(k):
+        if not me["via"]:
+            return
+        name, n = STAGES[k][0], PC * NH
+        rid, pid, _ = topo.addr(me["helper"])
+        for f in (0, 1):
+            before("g", [v(name + ("s" if f else "c"), 0, n)], [])
+            g.remote_dma(side(T, "rel%d" % k, f, 0, n), side(T, name, f, 0, n), T.sem[("rels%d" if f else "relc%d") % k],
+                         T.sem.sent, pid, rid, bits_of(me["heng"][f]))
+            sent[0] += len(me["heng"][f])
+
+    def to_ranks(k):
+        name = STAGES[k][0]
+        for f in (0, 1):
+            before("g", [v(name + ("s" if f else "c"), PC * NH, PC * (N - 1))], [])
+            sent[0] += pieces(g, T, topo, plan, r, me["self"], name, PC * NH, k, f)
+
+    def arrivals(k):
+        _, land, base = STAGES[k]
+        for f in (0, 1):
+            sem = ("arrs%d" if f else "arrc%d") % k
+            count[sem] = sum(len(plan[h]["eng"][r, f]) for h in range(N) if h != r)
+            note("r", sem, count[sem], [], [v(land + ("s" if f else "c"), base, base + PC * (N - 1))], {})
+
+    icol, capcol = v("bits", 0, 1), v("bits", 2, 3)
+    H = S // 2
+
+    dma("s", T.ein[:, 0:4 * H], T.e[:, 0:4 * H], [], [v("ein", 0, 4 * H)])
+    dma("a", T.xin[:, 0:512], T.x[:, 0:512], [], [v("xin", 0, 512)])
+    dma("s", T.ein[:, 4 * H:4 * S], T.e[:, 4 * H:4 * S], [], [v("ein", 4 * H, 4 * S)])
+    dma("a", T.pai[:], T.pa[:], [], [v("pai")])
+    dma("a", T.pbi[:], T.pb[:], [], [v("pbi")])
+    for t in (1, 2, 3):
+        dma("a" if t == 2 else "s", T.xin[:, 4 * W * t:4 * W * t + 512], T.x[:, 512 * t:512 * t + 512], [],
+            [v("xin", 4 * W * t, 4 * W * t + 512)])
+
+    iota(v("pci"), [[0, 1]], 0, 1, True)
+    iota(v("jm16"), [[0, 8], [1, 16]], 0)
+    iota(v("trow"), [[-32, 4]], 111)
+    iota(v("kmin"), [[-W, 4], [0, 2], [30000, 16]], 3 * W)
+    iota(v("gz"), [[0, 512]], 0)
+    iota(v("i448"), [[1, S]], 0)
+    iota(v("pcf"), [[0, 1]], 0, 1)
+    iota(v("t16"), [[CAP, 4]], 0)
+    iota(v("cb", 0, 6), [[S, 2], [0, 3]], 0)
+    iota(v("cb", 6, 12), [[S, 2], [2 * S, 3]], 2 * S)
+    iota(v("tli"), [[-1, 4], [0, 2]], 3, 0, True)
+    iota(v("j16"), [[16, 8]], 128)
+    iota(v("valrow"), [[PC, 8], [1, 16]], HW)
+    iota(v("inv", 128, 256), [[0, 128]], 0)
+    iota(v("rl", 0, 40), [[0, 40]], 128)
+    dma("g", T.vin[:], T.v[:], [], [v("vin")])
+
+    for t in range(TT):
+        memset(v("xin", 4 * W * t + 512, 4 * W * (t + 1)), 0.0)
+    for q in range(4):
+        for a in range(4):
+            memset(v("xa", a, a + 1, 1, 32 * q, 32 * q + 32), float(128 * ((q ^ a) >> 1) + 256 * ((q ^ a) & 1)))
+    ts(v("bitsi", 0, 1), v("pci"), 15, None, ALU.bitwise_and)
+    ts(v("bitsi", 1, 2), v("pci"), 4, 1, ALU.logical_shift_right, ALU.bitwise_and)
+    cp(v("bits", 0, 2), v("bitsi"))
+    for pos in range(N):
+        ts(v("ft", 4 * pos, 4 * pos + 4), v("trow"), v("xa", order[pos] >> 1, (order[pos] >> 1) + 1), float(16 * (order[pos] & 1)),
+           ALU.add, ALU.add)
+    ts(v("mask"), v("jm16"), icol, None, ALU.is_equal)
+    ts(v("rst"), v("jm16"), 0.5, None, ALU.is_ge)
+    ts(capcol, icol, 1.0, None, ALU.add)
+    tt(v("ft2"), v("ft"), v("mask", 0, 32), ALU.mult)
+    ts(v("cap"), v("mask"), 0.0, capcol, ALU.mult, ALU.add)
+    scan(v("ft3"), v("rst", 0, 32), v("ft2"), 0.0, ALU.mult, ALU.add)
+    cp(v("fl"), v("ft3", 15, 32, 16))
+    quant("qe", 0, H, "ein", 0)
+
+    def decode(x, stride, prep, first=None, late=None):
+        prep(0)
+        mm(0, x, 0, "qe", 0, H)
+        if first:
+            first()
+        mm(1, x, 0, "qe", H, H)
+        prep(1)
+        mm(2, x, stride, "qe", 0, S)
+        cp(v("aa", 0, H), v("ps0", 0, H))
+        acopy(v("aa", H, S), v("ps1", 0, H))
+        for t in (1, 2, 3):
+            prev = v("aa", S * (t - 1), S * t)
+            blocks = ((0, CUT), (CUT, S))
+            for a, b in blocks:
+                acopy(v("bt", 2 * S * t + a, 2 * S * t + b), prev, v("pau", a // 16, b // 16))
+            if t < 3:
+                prep(t + 1)
+                mm(t + 2, x, stride * (t + 1), "qe", 0, S)
+            elif late:
+                late()
+            for a, b in blocks:
+                m = v("bt", 2 * S * t + S + a, 2 * S * t + S + b)
+                tt(m, prev, v("bt", 2 * S * t + a, 2 * S * t + b), ALU.max, v("pbu", a // 16, b // 16))
+                tt(v("aa", S * t + a, S * t + b), m, v("ps%d" % (t + 1), a, b), ALU.add)
+        last = v("aa", 3 * S, 4 * S)
+        scan(v("rr"), last, last, -1.0e29, ALU.max, ALU.max)
+
+    top = v("rr", S - 1, S)
+
+    def trace(at):
+        below(v("path", at + 3, at + 4), v("rr"), top, S)
+        ts(v("bo", 8, 12), v("cb", 2, 12, 3), v("path", at + 3, at + 4), None, ALU.add)
+        for t in (3, 2, 1):
+            tt(v("gg"), v("bt"), v("mask", 0, 64), ALU.mult, v("bo", 4 * (t - 1), 4 * t))
+            scan(v("sc"), v("rst", 0, 64), v("gg"), 0.0, ALU.mult, ALU.add)
+            d = v("dd", t, t + 1)
+            ts(d, v("sc", 63, 64), v("sc", 47, 48), v("sc", 31, 32), ALU.is_gt, ALU.mult)
+            if t > 1:
+                ts(v("bo", 4 * (t - 2), 4 * (t - 1)), v("cb", t - 2, 12, 3), d, v("sc", 15, 16), ALU.add, ALU.add)
+            ts(v("path", at + t - 1, at + t), d, v("sc", 15, 16), None, ALU.add)
+
+    def spread(at, d0, init, op0):
+        transpose(v("tr"), v("mi"))
+        scan(v("gz", 0, 128), d0, v("tr"), init, op0, ALU.add)
+        cp(v("gz", 143, 256, 16, 64, 128), v("gz", 15, 128, 16, 0, 64))
+        cp(v("gz", 143, 256, 16, 0, 64), v("gz", 15, 128, 16, 64, 128))
+        for q in range(4):
+            o = q ^ 1
+            cp(v("gz", 271, 512, 16, 32 * q, 32 * q + 32), v("gz", 15, 256, 16, 32 * o, 32 * o + 32))
+        cp(v("offs", at, at + 32), v("gz"), v("fl"))
+
+    def slots(at):
+        below(v("dcol", 0, 1), v("rr", S // N - 1, S, S // N), top, N)
+        ts(v("db"), v("mask", 0, 32), 0.0, v("dcol", 0, 1), ALU.mult, ALU.add)
+        for a in range(4):
+            transpose(v("row", 32 * a, 32 * a + 32, 1, 0, 32), v("db", 0, 32, 1, 32 * a, 32 * a + 32))
+        for q in range(4):
+            ts(v("eq", 0, 128, 1, 32 * q, 32 * q + 32), v("row", 0, 128, 1, 0, 32), float(2 * q), v("bits", 1, 2, 1, 0, 32),
+               ALU.subtract, ALU.is_equal)
+        scan(v("cum"), v("eq"), v("cap"), 0.0, ALU.add, ALU.min)
+        below(v("dcol", 1, 2), v("cum"), capcol, 128)
+        ts(v("mi"), v("mask"), v("dcol", 1, 2), None, ALU.mult)
+        spread(at, v("kmin"), 1.0e9, ALU.min)
+
+    def homelist(at, base, stride):
+        w = [v("w8", 8 * k, 8 * k + 8) for k in range(8)]
+        cp(w[0], v("offs", at, at + 32, 4))
+        cp(v("inv", 0, 128), v("i448", 0, 128))
+        ts(w[1], w[0], 128.0, None, ALU.is_ge)
+        tt(w[2], w[1], v("j128"), ALU.mult)
+        tt(w[3], w[2], w[0], ALU.max)
+        cp(v("ro"), w[3])
+        inv, ro, val = v("inv"), v("ro"), v("valrow")
+        do("v", lambda: g.vector.tensor_copy(inv["ap"].indirect(ro["ap"]), val["ap"]), [ro, val], [inv])
+        tt(v("mi"), v("inv", 0, 128), v("mask"), ALU.mult)
+        scan(v("tr"), v("rst"), v("mi"), 0.0, ALU.mult, ALU.add)
+        b8 = v("tr", 15, 128, 16)
+        ts(w[4], b8, float(HW), float(CAP - W), ALU.is_ge, ALU.mult)
+        cp(v("rl", base, base + 8), b8)
+        for t in (1, 2, 3):
+            ts(w[4 + t], w[4], float(W), float(t), ALU.add, ALU.mult)
+        for t in (1, 2, 3):
+            tt(v("rl", base + stride * t, base + stride * t + 8), w[4 + t], b8, ALU.add)
+        cp(v("rlu", base, base + stride * TT), v("rl", base, base + stride * TT))
+
+    NA = max(128, PC * NH)
+    parts = ((0, NA, (5, 6, 7, 1)), (NA, 512, (0, 2, 3, 4)))
+
+    for turn in (1, 2):
+        held, win, out, land, xs, ep, new, nt = ["%s%d" % (n, turn) for n in ("held", "win", "out", "land", "xs", "ep", "new", "nt")]
+        k = 2 * turn - 1
+        if turn == 1:
+            def first():
+                quant("qe", H, S, "ein", H)
+                cp(v("pau"), v("pai"))
+                cp(v("pbu"), v("pbi"))
+            decode(held, W, lambda t: quant("held1", W * t, W * (t + 1), "xin", W * t), first)
+        else:
+            decode(held, W, lambda t: pick("held2", W * t, W * (t + 1), "win1", HW + 512, v("rlu", 10 * t, 10 * t + 9)))
+        move("s", win, 0, HW, held, 0)
+        fo = 64 * (turn - 1)
+        slots(fo)
+        if NH:
+            pick(out, 0, PC * NH, held, HW, v("offs", fo, fo + 4 * NH))
+            to_helper(k)
+        pick(out, PC * NH, PC * (N - 1), held, HW, v("offs", fo + 4 * NH, fo + 4 * (N - 1)))
+        to_ranks(k)
+        pick(land, PC * (N - 1), PC * N, held, HW, v("offs", fo + 4 * (N - 1), fo + 4 * N))
+        if turn == 1:
+            for h in range(N):
+                ts(v("xl", h, 32, 8), v("t16"), icol, float(PC * order.index(h)), ALU.add, ALU.add)
+            acopy(v("bt", 0, S), v("i448"), v("pau"))
+            memset(v("et"), 0.0)
+            for b in range(4):
+                ts(v("et", 512 * b + b, 512 * (b + 1), 4), v("i448", 0, 128), v("pcf"), None, ALU.is_equal)
+            tt(v("bt", S, 2 * S), v("i448"), v("bt", 0, S), ALU.subtract, v("pbu"))
+            quant("qk", 0, 512, "et", 0)
+            cp(v("tl"), v("tli"))
+            ts(v("j128"), v("j16"), icol, None, ALU.add)
+            quant("qv", 0, 128, "vin", 0)
+            homelist(fo, 0, 10)
+        else:
+            trace(0)
+            dma("s", T.ol[:], T.path[:, 0:4], [v("path", 0, 4)], [])
+            homelist(fo, 40, 8)
+        arrivals(k)
+
+        def held_part(part):
+            a, b, banks = part
+            for j in range(4):
+                mm(banks[j], "qk", 128 * j, land, a, b - a, True, False)
+        decode(xs, 128, lambda t: pick(xs, 128 * t, 128 * (t + 1), land, 512, v("xl", 8 * t, 8 * t + 8)),
+               None, lambda: held_part(parts[0]))
+        held_part(parts[1])
+        at = 8 * turn
+        trace(at)
+        tt(v("mi"), v("path", at, at + 4), v("mask"), ALU.mult, v("tl"))
+        if turn == 2:
+            dma("s", T.dl[:], T.path[:, at:at + 4], [v("path", at, at + 4)], [])
+        spread(fo + 32, v("rst"), 0.0, ALU.mult)
+        for a, b, banks in parts:
+            pick(ep, a, b, "qe", S, v("offs", fo + 32 + a // 16, fo + 32 + b // 16))
+            for j in range(4):
+                mm(banks[j], "qk", 128 * j, ep, a, b - a, False, True)
+        for a, b, banks in parts:
+            for j in (0, 2, 1, 3):
+                o, i = v(nt, 4 * a + j, 4 * b, 4), v("ps%d" % banks[j], 0, b - a)
+                if j < 2:
+                    ts(o, i, 0.5, None, ALU.mult)
+                else:
+                    do("a", lambda: g.scalar.activation(o["ap"], i["ap"], ACT.Copy, scale=0.5), [i], [o])
+            quant(new, a, b, nt, a)
+            if a == 0:
+                to_helper(k + 1)
+        to_ranks(k + 1)
+        move("s", win, HW + PC * (N - 1), HW + PC * N, new, PC * (N - 1))
+        arrivals(k + 1)
+
+    for j in (0, 1):
+        a, b = 256 * j, 256 * (j + 1)
+        pick("fin", a, b, "win2", HW + 512, v("rlu", 40 + 16 * j, 56 + 16 * j))
+        mm(5 + j, "qv", 0, "fin", a, 256)
+        dma("s", T.oc[:, 4 * a:4 * b], side(T, "fin", 0, a, b), [v("finc", a, b)], [])
+    cp(v("ysb", 0, 256), v("ps5", 0, 256))
+    dma("s", T.y[:, 0:256], T.ysb[:, 0:256], [v("ysb", 0, 256)], [])
+    acopy(v("ysb", 256, 512), v("ps6", 0, 256))
+    dma("a", T.y[:, 256:512], T.ysb[:, 256:512], [v("ysb", 256, 512)], [])
+    for q in range(4):
+        dma("s" if q < 2 else "a", T.osc[4 * q:4 * q + 4, :], T.fins[32 * q:32 * q + 4, :], [v("fins", 0, 512, 1, 32 * q, 32 * q + 4)], [])
+
+    count["sent"] = sent[0]
+    for sem in count:
+        if waited.get(sem, 0) < count[sem]:
+            g.wait_ge(T.sem[sem], count[sem])

@@ -1,5 +1,5 @@
 from concourse.bass import DstId, RemoteDMATransfer
-from concourse.mybir import dt, AluOpType, ActivationFunctionType
+from concourse.mybir import dt, AluOpType, ActivationFunctionType, AxisListType
 
 ALU = AluOpType
 ACT = ActivationFunctionType
@@ -8,36 +8,22 @@ W = 144
 HW = TT * W
 PC = TT * CAP
 NH = 2
-CUT = 160
+B1, B2, B3 = (0, 128), (128, 288), (288, S)
 C4, U8 = "float8_e4m3fn_x4", "uint8"
 
-SCRATCH = {
-    "xin": ("sbuf", [128, 4 * HW], "bfloat16"), "ein": ("sbuf", [128, 4 * S], "bfloat16"), "vin": ("sbuf", [128, 512], "bfloat16"),
-    "pai": ("sbuf", [128, 28], "int32"), "pbi": ("sbuf", [128, 28], "int32"),
-    "pau": ("sbuf", [128, 28], "uint16"), "pbu": ("sbuf", [128, 28], "uint16"),
-    "et": ("sbuf", [128, 2048], "bfloat16"), "nt1": ("sbuf", [128, 2048], "bfloat16"), "nt2": ("sbuf", [128, 2048], "bfloat16"),
-    "aa": ("sbuf", [128, TT * S], "float32"), "bt": ("sbuf", [128, 8 * S], "float32"), "rr": ("sbuf", [128, S], "float32"),
-    "junk": ("sbuf", [128, S], "float32"), "ysb": ("sbuf", [128, 512], "float32"),
-    "pci": ("sbuf", [128, 1], "int32"), "pcf": ("sbuf", [128, 1], "float32"), "bitsi": ("sbuf", [128, 2], "int32"),
-    "bits": ("sbuf", [128, 4], "float32"), "jm16": ("sbuf", [128, 128], "float32"), "mask": ("sbuf", [128, 128], "float32"),
-    "rst": ("sbuf", [128, 128], "float32"), "kmin": ("sbuf", [128, 128], "float32"), "cap": ("sbuf", [128, 128], "bfloat16"),
-    "i448": ("sbuf", [128, S], "float32"), "trow": ("sbuf", [128, 4], "float32"), "xa": ("sbuf", [128, 4], "float32"),
-    "ft": ("sbuf", [128, 32], "float32"), "ft2": ("sbuf", [128, 32], "float32"), "ft3": ("sbuf", [128, 32], "float32"),
-    "fl": ("sbuf", [128, 2], "uint16"), "gz": ("sbuf", [128, 512], "float32"), "mi": ("sbuf", [128, 128], "float32"),
-    "tr": ("sbuf", [128, 128], "float32"), "dcol": ("sbuf", [128, 2], "float32"), "db": ("sbuf", [128, 32], "bfloat16"),
-    "row": ("sbuf", [128, 128], "bfloat16"), "eq": ("sbuf", [128, 128], "bfloat16"), "cum": ("sbuf", [128, 128], "bfloat16"),
-    "offs": ("sbuf", [128, 128], "uint16"), "t16": ("sbuf", [128, 4], "float32"), "xl": ("sbuf", [128, 32], "uint16"),
-    "cb": ("sbuf", [128, 12], "float32"), "tli": ("sbuf", [128, 8], "int32"), "tl": ("sbuf", [128, 8], "uint16"),
-    "j16": ("sbuf", [128, 8], "float32"), "j128": ("sbuf", [128, 8], "float32"), "valrow": ("sbuf", [128, 128], "float32"),
-    "inv": ("sbuf", [128, 256], "float32"), "w8": ("sbuf", [128, 64], "float32"), "ro": ("sbuf", [128, 8], "uint16"),
-    "rl": ("sbuf", [128, 80], "float32"), "rlu": ("sbuf", [128, 80], "uint16"),
-    "bo": ("sbuf", [128, 12], "uint16"), "gg": ("sbuf", [128, 64], "float32"), "sc": ("sbuf", [128, 64], "float32"),
-    "dd": ("sbuf", [128, 4], "float32"), "path": ("sbuf", [128, 24], "float32"),
-}
+SCRATCH = {}
+for _d, _l in (("bfloat16", "xin 2304 ein 1792 vin 512 et 2048 nt1 2048 nt2 2048 cap 128 db 32 row 128 eq 128 cum 128"),
+               ("int32", "pai 28 pbi 28 pci 1 bitsi 2 tli 8"),
+               ("uint16", "pau 28 pbu 28 fl 2 offs 128 xl 32 tl 8 ro 8 rlu 80 bo 12 ownl 4"),
+               ("float32", "aa 1792 bt 3584 rr 448 junk 448 lt 160 ysb 512 pcf 1 bits 4 jm16 128 mask 128 rst 128 kmin 128 i448 448 "
+                           "trow 4 xa 4 ft 32 ft2 32 ft3 32 gz 512 mi 128 tr 128 dcol 4 t16 4 cb 12 j16 8 j128 8 valrow 128 "
+                           "inv 256 w8 64 rl 80 gg 64 sc 64 dd 4 path 24")):
+    _l = _l.split()
+    for _k in range(0, len(_l), 2):
+        SCRATCH[_l[_k]] = ("sbuf", [128, int(_l[_k + 1])], _d)
 for _n, _w in (("qe", S), ("qv", 128), ("qk", 512), ("held1", HW), ("held2", HW), ("win1", HW + 512), ("win2", HW + 512),
                ("out1", 512), ("out2", 512), ("land1", 512), ("land2", 512), ("xs1", 512), ("xs2", 512), ("ep1", 512), ("ep2", 512),
-               ("new1", 512), ("new2", 512), ("fin", 512),
-               ("rel1", PC * max(NH, 1)), ("rel2", PC * max(NH, 1)), ("rel3", PC * max(NH, 1)), ("rel4", PC * max(NH, 1))):
+               ("new1", 512), ("new2", 512), ("fin", 512), ("rel1", PC * NH), ("rel2", PC * NH), ("rel3", PC * NH), ("rel4", PC * NH)):
     SCRATCH[_n + "c"] = ("sbuf", [128, _w], C4)
     SCRATCH[_n + "s"] = ("sbuf", [128, _w], U8)
 for _b in range(8):
@@ -97,10 +83,9 @@ def routes(cores, topo):
                 eng[d, f] = m
             for d, m in zip(sib, deal(len(sib), in_engs, f)):
                 eng[d, f] = m
-            if via:
-                for d, m in zip(via, deal(len(via), topo.engines(helper, cores[via[0]]), f)):
-                    eng[d, f] = m
-        plan.append({"order": via + direct + sib + [r], "via": via, "self": direct + sib, "helper": helper, "eng": eng,
+            for d, m in zip(via, deal(len(via), topo.engines(helper, cores[via[0]]), f)):
+                eng[d, f] = m
+        plan.append({"order": via + direct + sib + [r], "via": via, "direct": direct, "sib": sib, "helper": helper, "eng": eng,
                      "heng": (topo.engines(c, helper), in_engs)})
     return plan
 
@@ -138,7 +123,7 @@ def rank_program(g, core, T, topo):
     r = T.rank_of(core)
     if r is None:
         for k in range(N):
-            if plan[k]["via"] and plan[k]["helper"] == core:
+            if plan[k]["helper"] == core:
                 helper_program(g, T, topo, plan, k)
         return
     me = plan[r]
@@ -254,52 +239,46 @@ def rank_program(g, core, T, topo):
         c, s, t = v(name + "c", a, b), v(name + "s", a, b), v(tile, 4 * ta, 4 * (ta + b - a))
         do("v", lambda: g.vector.quantize_mx(c["ap"], s["ap"], t["ap"]), [t], [c, s])
 
-    def pickc(dst, a, b, win, n, off):
+    def pick(dst, a, b, win, n, off):
         o, w = v(dst + "c", a, b), v(win + "c", 0, n)
         do("v", lambda: g.vector.tensor_copy(o["ap"].bitcast(dt.uint32), w["ap"].bitcast(dt.uint32).indirect(off["ap"])), [w, off], [o])
-
-    def picks(dst, a, b, win, n, off):
         acopy(v(dst + "s", a, b), v(win + "s", 0, n), off)
-
-    def pick(dst, a, b, win, n, off):
-        pickc(dst, a, b, win, n, off)
-        picks(dst, a, b, win, n, off)
 
     def mm(bank, w, wa, x, xa, n, start=True, stop=True):
         o = v("ps%d" % bank, 0, n)
         wc, ws, xc, xs = v(w + "c", wa, wa + 128), v(w + "s", wa, wa + 128), v(x + "c", xa, xa + n), v(x + "s", xa, xa + n)
         do("p", lambda: g.tensor.matmul_mx(o["ap"], wc["ap"], ws["ap"], xc["ap"], xs["ap"], start, stop), [wc, ws, xc, xs], [o])
 
-    def move(e, dst, a, b, from_, fa):
-        for f in (0, 1):
-            x = "s" if f else "c"
-            dma(e, side(T, dst, f, a, b), side(T, from_, f, fa, fa + b - a), [v(from_ + x, fa, fa + b - a)], [v(dst + x, a, b)])
-
     sent = [0]
+    CH, CD, CS = PC * NH, PC * (NH + len(me["direct"])), PC * (N - 1)
 
-    def to_helper(k):
-        if not me["via"]:
-            return
-        name, n = STAGES[k][0], PC * NH
-        rid, pid, _ = topo.addr(me["helper"])
-        for f in (0, 1):
-            before("g", [v(name + ("s" if f else "c"), 0, n)], [])
-            g.remote_dma(side(T, "rel%d" % k, f, 0, n), side(T, name, f, 0, n), T.sem[("rels%d" if f else "relc%d") % k],
-                         T.sem.sent, pid, rid, bits_of(me["heng"][f]))
-            sent[0] += len(me["heng"][f])
-
-    def to_ranks(k):
+    def to_helper(k, f):
         name = STAGES[k][0]
-        for f in (0, 1):
-            before("g", [v(name + ("s" if f else "c"), PC * NH, PC * (N - 1))], [])
-            sent[0] += pieces(g, T, topo, plan, r, me["self"], name, PC * NH, k, f)
+        rid, pid, _ = topo.addr(me["helper"])
+        before("g", [v(name + ("s" if f else "c"), 0, CH)], [])
+        g.remote_dma(side(T, "rel%d" % k, f, 0, CH), side(T, name, f, 0, CH), T.sem[("rels%d" if f else "relc%d") % k],
+                     T.sem.sent, pid, rid, bits_of(me["heng"][f]))
+        sent[0] += len(me["heng"][f])
+
+    def to_ranks(k, f, dests, a):
+        name = STAGES[k][0]
+        before("g", [v(name + ("s" if f else "c"), a, a + PC * len(dests))], [])
+        sent[0] += pieces(g, T, topo, plan, r, dests, name, a, k, f)
+
+    def sends(k):
+        to_helper(k, 0)
+        to_ranks(k, 0, me["direct"], CH)
+        to_helper(k, 1)
+        to_ranks(k, 1, me["direct"], CH)
+        to_ranks(k, 0, me["sib"], CD)
+        to_ranks(k, 1, me["sib"], CD)
 
     def arrivals(k):
         _, land, base = STAGES[k]
         for f in (0, 1):
             sem = ("arrs%d" if f else "arrc%d") % k
             count[sem] = sum(len(plan[h]["eng"][r, f]) for h in range(N) if h != r)
-            note("r", sem, count[sem], [], [v(land + ("s" if f else "c"), base, base + PC * (N - 1))], {})
+            note("r", sem, count[sem], [], [v(land + ("s" if f else "c"), base, base + CS)], {})
 
     icol, capcol = v("bits", 0, 1), v("bits", 2, 3)
     H = S // 2
@@ -362,26 +341,38 @@ def rank_program(g, core, T, topo):
         acopy(v("aa", H, S), v("ps1", 0, H))
         for t in (1, 2, 3):
             prev = v("aa", S * (t - 1), S * t)
-            blocks = ((0, CUT), (CUT, S))
-            for a, b in blocks:
+            for a, b in (B1, B2, B3):
                 acopy(v("bt", 2 * S * t + a, 2 * S * t + b), prev, v("pau", a // 16, b // 16))
             if t < 3:
                 prep(t + 1)
                 mm(t + 2, x, stride * (t + 1), "qe", 0, S)
             elif late:
                 late()
-            for a, b in blocks:
-                m = v("bt", 2 * S * t + S + a, 2 * S * t + S + b)
-                tt(m, prev, v("bt", 2 * S * t + a, 2 * S * t + b), ALU.max, v("pbu", a // 16, b // 16))
-                tt(v("aa", S * t + a, S * t + b), m, v("ps%d" % (t + 1), a, b), ALU.add)
+
+            def larger(a, b):
+                tt(v("bt", 2 * S * t + S + a, 2 * S * t + S + b), prev, v("bt", 2 * S * t + a, 2 * S * t + b), ALU.max,
+                   v("pbu", a // 16, b // 16))
+
+            def add(a, b):
+                tt(v("aa", S * t + a, S * t + b), v("bt", 2 * S * t + S + a, 2 * S * t + S + b), v("ps%d" % (t + 1), a, b), ALU.add)
+            larger(*B1)
+            larger(*B2)
+            add(*B1)
+            larger(*B3)
+            add(*B2)
+            add(*B3)
         last = v("aa", 3 * S, 4 * S)
         scan(v("rr"), last, last, -1.0e29, ALU.max, ALU.max)
 
     top = v("rr", S - 1, S)
 
     def trace(at):
-        below(v("path", at + 3, at + 4), v("rr"), top, S)
-        ts(v("bo", 8, 12), v("cb", 2, 12, 3), v("path", at + 3, at + 4), None, ALU.add)
+        sa, sb, lt = v("dcol", 2, 3), v("dcol", 3, 4), v("lt")
+        below(sa, v("rr", 0, S - 160), top, S - 160)
+        ts(lt, v("rr", S - 160, S), top, None, ALU.is_lt)
+        do("v", lambda: g.vector.tensor_reduce(sb["ap"], lt["ap"], AxisListType.X, ALU.add), [lt], [sb])
+        ts(v("bo", 8, 12), v("cb", 2, 12, 3), sa, sb, ALU.add, ALU.add)
+        ts(v("path", at + 3, at + 4), sa, sb, None, ALU.add)
         for t in (3, 2, 1):
             tt(v("gg"), v("bt"), v("mask", 0, 64), ALU.mult, v("bo", 4 * (t - 1), 4 * t))
             scan(v("sc"), v("rst", 0, 64), v("gg"), 0.0, ALU.mult, ALU.add)
@@ -396,7 +387,7 @@ def rank_program(g, core, T, topo):
         scan(v("gz", 0, 128), d0, v("tr"), init, op0, ALU.add)
         cp(v("gz", 143, 256, 16, 64, 128), v("gz", 15, 128, 16, 0, 64))
         cp(v("gz", 143, 256, 16, 0, 64), v("gz", 15, 128, 16, 64, 128))
-        for q in range(4):
+        for q in (3, 2, 1, 0):
             o = q ^ 1
             cp(v("gz", 271, 512, 16, 32 * q, 32 * q + 32), v("gz", 15, 256, 16, 32 * o, 32 * o + 32))
         cp(v("offs", at, at + 32), v("gz"), v("fl"))
@@ -435,8 +426,7 @@ def rank_program(g, core, T, topo):
             tt(v("rl", base + stride * t, base + stride * t + 8), w[4 + t], b8, ALU.add)
         cp(v("rlu", base, base + stride * TT), v("rl", base, base + stride * TT))
 
-    NA = max(128, PC * NH)
-    parts = ((0, NA, (5, 6, 7, 1)), (NA, 512, (0, 2, 3, 4)))
+    parts = ((0, CH, (5, 6, 7, 1)), (CH, 512, (0, 2, 3, 4)))
 
     for turn in (1, 2):
         held, win, out, land, xs, ep, new, nt = ["%s%d" % (n, turn) for n in ("held", "win", "out", "land", "xs", "ep", "new", "nt")]
@@ -449,15 +439,15 @@ def rank_program(g, core, T, topo):
             decode(held, W, lambda t: quant("held1", W * t, W * (t + 1), "xin", W * t), first)
         else:
             decode(held, W, lambda t: pick("held2", W * t, W * (t + 1), "win1", HW + 512, v("rlu", 10 * t, 10 * t + 9)))
-        move("s", win, 0, HW, held, 0)
+        for f in (0, 1):
+            x = "s" if f else "c"
+            dma("s", side(T, win, f, 0, HW), side(T, held, f, 0, HW), [v(held + x)], [v(win + x, 0, HW)])
         fo = 64 * (turn - 1)
         slots(fo)
-        if NH:
-            pick(out, 0, PC * NH, held, HW, v("offs", fo, fo + 4 * NH))
-            to_helper(k)
-        pick(out, PC * NH, PC * (N - 1), held, HW, v("offs", fo + 4 * NH, fo + 4 * (N - 1)))
-        to_ranks(k)
-        pick(land, PC * (N - 1), PC * N, held, HW, v("offs", fo + 4 * (N - 1), fo + 4 * N))
+        for a, b in ((0, CH), (CH, CD), (CD, CS)):
+            pick(out, a, b, held, HW, v("offs", fo + a // 16, fo + b // 16))
+        sends(k)
+        pick(land, CS, 512, held, HW, v("offs", fo + CS // 16, fo + 32))
         if turn == 1:
             for h in range(N):
                 ts(v("xl", h, 32, 8), v("t16"), icol, float(PC * order.index(h)), ALU.add, ALU.add)
@@ -469,13 +459,15 @@ def rank_program(g, core, T, topo):
             quant("qk", 0, 512, "et", 0)
             cp(v("tl"), v("tli"))
             ts(v("j128"), v("j16"), icol, None, ALU.add)
+            ts(v("ownl"), v("t16"), icol, float(CS), ALU.add, ALU.add)
             quant("qv", 0, 128, "vin", 0)
             homelist(fo, 0, 10)
         else:
             trace(0)
-            dma("s", T.ol[:], T.path[:, 0:4], [v("path", 0, 4)], [])
             homelist(fo, 40, 8)
         arrivals(k)
+        if turn == 2:
+            dma("s", T.ol[:], T.path[:, 0:4], [v("path", 0, 4), v(land + "s")], [])
 
         def held_part(part):
             a, b, banks = part
@@ -494,18 +486,16 @@ def rank_program(g, core, T, topo):
             pick(ep, a, b, "qe", S, v("offs", fo + 32 + a // 16, fo + 32 + b // 16))
             for j in range(4):
                 mm(banks[j], "qk", 128 * j, ep, a, b - a, False, True)
-        for a, b, banks in parts:
+        for a, b, part in ((0, CH, parts[0]), (CH, CD, parts[1]), (CD, 512, parts[1])):
             for j in (0, 2, 1, 3):
-                o, i = v(nt, 4 * a + j, 4 * b, 4), v("ps%d" % banks[j], 0, b - a)
+                o, i = v(nt, 4 * a + j, 4 * b, 4), v("ps%d" % part[2][j], a - part[0], b - part[0])
                 if j < 2:
                     ts(o, i, 0.5, None, ALU.mult)
                 else:
                     do("a", lambda: g.scalar.activation(o["ap"], i["ap"], ACT.Copy, scale=0.5), [i], [o])
             quant(new, a, b, nt, a)
-            if a == 0:
-                to_helper(k + 1)
-        to_ranks(k + 1)
-        move("s", win, HW + PC * (N - 1), HW + PC * N, new, PC * (N - 1))
+        sends(k + 1)
+        pick(win, HW + CS, HW + 512, new, 512, v("ownl"))
         arrivals(k + 1)
 
     for j in (0, 1):

@@ -7,17 +7,22 @@ N, TT, S, CAP = 8, 4, 448, 16
 W = 144
 HW = TT * W
 PC = TT * CAP
-NH = 2
+NH = 4
 B1, B2, B3 = (0, 128), (128, 288), (288, S)
 C4, U8 = "float8_e4m3fn_x4", "uint8"
+CS = PC * (N - 1)
+PICKS = {1: ((128, 384), (0, 128), (384, CS)), 2: ((0, 256), (256, CS))}
+CH = 256
+SUBS = ((0, 256), (256, 512))
 
 SCRATCH = {}
-for _d, _l in (("bfloat16", "xin 2304 ein 1792 vin 512 et 2048 nt1 2048 nt2 2048 cap 128 db 32 row 128 eq 128 cum 128"),
-               ("int32", "pai 28 pbi 28 pci 1 bitsi 2 tli 8"),
-               ("uint16", "pau 28 pbu 28 fl 2 offs 128 xl 32 tl 8 ro 8 rlu 80 bo 12 ownl 4"),
-               ("float32", "aa 1792 bt 3584 rr 448 junk 448 lt 160 ysb 512 pcf 1 bits 4 jm16 128 mask 128 rst 128 kmin 128 i448 448 "
-                           "trow 4 xa 4 ft 32 ft2 32 ft3 32 gz 512 mi 128 tr 128 dcol 4 t16 4 cb 12 j16 8 j128 8 valrow 128 "
-                           "inv 256 w8 64 rl 80 gg 64 sc 64 dd 4 path 24")):
+for _d, _l in (("bfloat16", "xin 2304 ein 1792 vin 512 et 2048 nt1 2048 nt2 2048 cap 128 db 32 row 128 eq 128 cum 128 "
+                            "maskb 128 mib 128 trb 128"),
+               ("int32", "pai 28 pbi 28 pci 1 bitsi 4"),
+               ("uint16", "pau 28 pbu 28 fl 2 offs 128 xl 32 ro 8 rlu 80 bo 12 ownl 4"),
+               ("float32", "aa 1792 bt 3584 rr 448 junk 448 lt 160 ysb 512 pcf 1 bits 5 jm16 128 mask 128 rst 128 kmin 128 i448 448 "
+                           "trow 8 ab 8 xa 12 ft 32 ft2 32 ft3 32 gz 512 mi 128 tr 128 dcol 4 t16 4 cb 12 j16 8 j128 8 valrow 128 "
+                           "inv 256 w8 64 rl 80 gg 64 sc 64 dd 4 path 24 off32 32 cut 128")):
     _l = _l.split()
     for _k in range(0, len(_l), 2):
         SCRATCH[_l[_k]] = ("sbuf", [128, int(_l[_k + 1])], _d)
@@ -29,7 +34,7 @@ for _n, _w in (("qe", S), ("qv", 128), ("qk", 512), ("held1", HW), ("held2", HW)
 for _b in range(8):
     SCRATCH["ps%d" % _b] = ("psum", [128, 512], "float32")
 
-SEMAPHORES = (["cv", "ca", "cp", "cg", "sent"] + ["%s%d" % (a, k) for a in ("arrc", "arrs", "relc", "rels") for k in range(1, 5)]
+SEMAPHORES = (["cv", "ca", "cp", "cg", "sent"] + ["%s%d" % (a, k) for a in ("arrc", "arrs", "rel0", "rel1") for k in range(1, 5)]
               + ["d%d" % k for k in range(40)])
 
 STAGES = {1: ("out1", "land1", 0), 2: ("new1", "win1", HW), 3: ("out2", "land2", 0), 4: ("new2", "win2", HW)}
@@ -42,51 +47,60 @@ def bits_of(engs):
     return m
 
 
-def deal(n, engs, flip):
-    sizes = [1] * n
-    while True:
-        k = sizes.index(min(sizes))
-        if sum(sizes) + sizes[k] > len(engs):
-            break
-        sizes[k] *= 2
-    if flip:
-        sizes = sizes[::-1]
-    out, at = [], 0
-    for s in sizes:
-        out.append(engs[at:at + s])
-        at += s
-    return out
+def deal(n, engs):
+    s = len(engs) // n
+    return [engs[s * k:s * (k + 1)] for k in range(n)]
 
 
 def routes(cores, topo):
+    def on_chip(ch):
+        return [k for k in range(N) if topo.chip(cores[k]) == ch]
+
+    def far_chips(ch):
+        return sorted({topo.chip(c) for c in cores if topo.chip(c) != ch and not topo.same_plane(ch, topo.chip(c))})
+
+    def helpers(r):
+        c = cores[r]
+        far = cores[on_chip(far_chips(topo.chip(c))[0])[0]]
+        free = [k for k in topo.cores_of(c) if k not in cores]
+        hx = [k for k in free if topo.may_write(k, far)]
+        hp = [k for k in free if k not in hx and topo.die(k) != topo.die(c)]
+        hq = [k for k in free if k not in hx and k not in hp]
+        place = on_chip(topo.chip(c)).index(r)
+        return hx[place], hp[place], hq[place]
+
     plan = []
     for r, c in enumerate(cores):
-        here = [k for k in range(N) if topo.chip(cores[k]) == topo.chip(c)]
-        sib = [k for k in here if k != r]
-        off = [k for k in range(N) if k not in here]
+        ch = topo.chip(c)
+        here = on_chip(ch)
+        near = [k for k in range(N) if topo.same_plane(ch, topo.chip(cores[k]))]
+        far = far_chips(ch)
+        y1, y2 = far[here.index(r)], far[1 - here.index(r)]
+        hx, hp, hq = helpers(r)
+        order = near + on_chip(y1) + on_chip(y2) + [k for k in here if k != r] + [r]
+        lo = topo.engines(c, cores[near[0]])
+        hi = [e for e in topo.engines(c, hq) if e not in lo]
 
-        def place(k):
-            return [j for j in range(N) if topo.chip(cores[j]) == topo.chip(cores[k])].index(k)
-        like = [k for k in off if place(k) == place(r)]
-        like = ([k for k in like if not topo.same_plane(topo.chip(c), topo.chip(cores[k]))]
-                + [k for k in like if topo.same_plane(topo.chip(c), topo.chip(cores[k]))])
-        via = like[:NH]
-        direct = [k for k in off if k not in via]
-        cands = [k for k in topo.cores_of(c) if k not in cores and topo.die(k) != topo.die(c)
-                 and all(topo.may_write(k, cores[d]) for d in via)]
-        helper = cands[place(r)]
-        out_engs = topo.engines(c, cores[direct[0]])
-        in_engs = [e for e in topo.engines(c, cores[sib[0]]) if e not in out_engs]
-        eng = {}
-        for f in (0, 1):
-            for d, m in zip(direct, deal(len(direct), out_engs, f)):
-                eng[d, f] = m
-            for d, m in zip(sib, deal(len(sib), in_engs, f)):
-                eng[d, f] = m
-            for d, m in zip(via, deal(len(via), topo.engines(helper, cores[via[0]]), f)):
-                eng[d, f] = m
-        plan.append({"order": via + direct + sib + [r], "via": via, "direct": direct, "sib": sib, "helper": helper, "eng": eng,
-                     "heng": (topo.engines(c, helper), in_engs)})
+        def direct(a, engs, n=2):
+            return [(a + j, 1, None, m, 0) for j, m in enumerate(deal(n, engs))]
+        out = [(0, [(0, 2, hp, hi, 0), (2, 2, hx, lo, 0)]), (1, [(0, 2, hq, hi, 0)]),
+               (0, direct(4, lo) + direct(6, hi, 1)), (1, direct(2, lo, 4) + direct(6, hi, 1))]
+        half = deal(2, hi)
+        first = [(0, direct(2, lo, 4)), (0, [(0, 2, hp, hi, 0)]), (1, [(0, 2, hq, half[0], 0), (2, 2, hx, half[1], 0)]),
+                 (1, direct(4, lo) + direct(6, hi, 1)), (0, direct(6, hi, 1))]
+        ways = []
+        for calls in (first, out, out, out):
+            eng, relay = {}, []
+            for f, trs in calls:
+                for a, n, to, e, slot in trs:
+                    if to is None:
+                        eng[order[a], f] = e
+                    else:
+                        relay.append((slot, to, f, a, n, len(e)))
+                        for j, m in enumerate(deal(n, topo.engines(to, cores[order[a]]))):
+                            eng[order[a + j], f] = m
+            ways.append({"calls": calls, "relay": relay, "eng": eng})
+        plan.append({"order": order, "ways": ways})
     return plan
 
 
@@ -94,37 +108,40 @@ def side(T, name, f, a, b):
     return T[name + "s"][:, a:b] if f else T[name + "c"][:, a:b].bitcast(dt.uint8)
 
 
-def pieces(g, T, topo, plan, r, dests, src, at, k, f):
+def landing(T, plan, r, d, k, f):
     _, land, base = STAGES[k]
-    trs, n = [], 0
-    for j, d in enumerate(dests):
-        rid, pid, _ = topo.addr(T.cores[d])
-        c = base + PC * plan[d]["order"].index(r)
-        e = plan[r]["eng"][d, f]
-        trs.append(RemoteDMATransfer(dst_ids=[DstId(rid=rid, pnc=pid)], dma_engine_mask=bits_of(e),
-                                     remote_sem=T.sem[("arrs%d" if f else "arrc%d") % k],
-                                     src=side(T, src, f, at + PC * j, at + PC * (j + 1)), dst=side(T, land, f, c, c + PC)))
-        n += len(e)
-    g.remote_dma_fused(trs, local_sem=T.sem.sent)
-    return n
+    c = base + PC * plan[d]["order"].index(r)
+    return side(T, land, f, c, c + PC), T.sem[("arrs%d" if f else "arrc%d") % k]
 
 
-def helper_program(g, T, topo, plan, r):
-    n = 0
+def transfer(topo, core, engs, src, dst, sem):
+    rid, pid, _ = topo.addr(core)
+    return RemoteDMATransfer(dst_ids=[DstId(rid=rid, pnc=pid)], dma_engine_mask=bits_of(engs), remote_sem=sem, src=src, dst=dst)
+
+
+def helper_program(g, T, topo, plan, core):
+    sent = 0
     for k in range(1, 5):
-        for f in (0, 1):
-            g.wait_ge(T.sem[("rels%d" if f else "relc%d") % k], len(plan[r]["heng"][f]))
-            n += pieces(g, T, topo, plan, r, plan[r]["via"], "rel%d" % k, 0, k, f)
-    g.wait_ge(T.sem.sent, n)
+        for (slot, _, f, a, n, count), r in sorted((j, r) for r in range(N) for j in plan[r]["ways"][k - 1]["relay"] if j[1] == core):
+            eng = plan[r]["ways"][k - 1]["eng"]
+            g.wait_ge(T.sem["rel%d%d" % (slot, k)], count)
+            trs = []
+            for j in range(n):
+                d = plan[r]["order"][a + j]
+                dst, sem = landing(T, plan, r, d, k, f)
+                at = PC * (2 * slot + j)
+                trs.append(transfer(topo, T.cores[d], eng[d, f], side(T, "rel%d" % k, f, at, at + PC), dst, sem))
+                sent += len(eng[d, f])
+            g.remote_dma_fused(trs, local_sem=T.sem.sent)
+    if sent:
+        g.wait_ge(T.sem.sent, sent)
 
 
 def rank_program(g, core, T, topo):
     plan = routes(list(T.cores), topo)
     r = T.rank_of(core)
     if r is None:
-        for k in range(N):
-            if plan[k]["helper"] == core:
-                helper_program(g, T, topo, plan, k)
+        helper_program(g, T, topo, plan, core)
         return
     me = plan[r]
     order = me["order"]
@@ -215,6 +232,9 @@ def rank_program(g, core, T, topo):
     def scan(out, d0, d1, init, op0, op1):
         do("v", lambda: g.vector.tensor_tensor_scan(out["ap"], d0["ap"], d1["ap"], init, op0, op1), [d0, d1], [out])
 
+    def reduce(out, in_, op):
+        do("v", lambda: g.vector.tensor_reduce(out["ap"], in_["ap"], AxisListType.X, op), [in_], [out])
+
     def transpose(out, in_):
         do("v", lambda: g.vector.transpose(out["ap"], in_["ap"]), [in_], [out])
 
@@ -250,51 +270,50 @@ def rank_program(g, core, T, topo):
         do("p", lambda: g.tensor.matmul_mx(o["ap"], wc["ap"], ws["ap"], xc["ap"], xs["ap"], start, stop), [wc, ws, xc, xs], [o])
 
     sent = [0]
-    CH, CD, CS = PC * NH, PC * (NH + len(me["direct"])), PC * (N - 1)
-
-    def to_helper(k, f):
-        name = STAGES[k][0]
-        rid, pid, _ = topo.addr(me["helper"])
-        before("g", [v(name + ("s" if f else "c"), 0, CH)], [])
-        g.remote_dma(side(T, "rel%d" % k, f, 0, CH), side(T, name, f, 0, CH), T.sem[("rels%d" if f else "relc%d") % k],
-                     T.sem.sent, pid, rid, bits_of(me["heng"][f]))
-        sent[0] += len(me["heng"][f])
-
-    def to_ranks(k, f, dests, a):
-        name = STAGES[k][0]
-        before("g", [v(name + ("s" if f else "c"), a, a + PC * len(dests))], [])
-        sent[0] += pieces(g, T, topo, plan, r, dests, name, a, k, f)
 
     def sends(k):
-        to_helper(k, 0)
-        to_ranks(k, 0, me["direct"], CH)
-        to_helper(k, 1)
-        to_ranks(k, 1, me["direct"], CH)
-        to_ranks(k, 0, me["sib"], CD)
-        to_ranks(k, 1, me["sib"], CD)
+        name = STAGES[k][0]
+        for f, trs in me["ways"][k - 1]["calls"]:
+            x = "s" if f else "c"
+            before("g", [v(name + x, PC * a, PC * (a + n)) for a, n, to, e, slot in trs], [])
+            out = []
+            for a, n, to, e, slot in trs:
+                if to is None:
+                    dst, sem = landing(T, plan, r, order[a], k, f)
+                    to = T.cores[order[a]]
+                else:
+                    dst, sem = side(T, "rel%d" % k, f, 2 * PC * slot, PC * (2 * slot + n)), T.sem["rel%d%d" % (slot, k)]
+                out.append(transfer(topo, to, e, side(T, name, f, PC * a, PC * (a + n)), dst, sem))
+                sent[0] += len(e)
+            g.remote_dma_fused(out, local_sem=T.sem.sent)
 
     def arrivals(k):
         _, land, base = STAGES[k]
         for f in (0, 1):
             sem = ("arrs%d" if f else "arrc%d") % k
-            count[sem] = sum(len(plan[h]["eng"][r, f]) for h in range(N) if h != r)
+            count[sem] = sum(len(plan[h]["ways"][k - 1]["eng"][r, f]) for h in range(N) if h != r)
             note("r", sem, count[sem], [], [v(land + ("s" if f else "c"), base, base + CS)], {})
 
-    icol, capcol = v("bits", 0, 1), v("bits", 2, 3)
-    H = S // 2
+    icol, capcol = v("bits", 0, 1), v("bits", 4, 5)
+    H, H1 = S // 2, 320
 
-    dma("s", T.ein[:, 0:4 * H], T.e[:, 0:4 * H], [], [v("ein", 0, 4 * H)])
-    dma("a", T.xin[:, 0:512], T.x[:, 0:512], [], [v("xin", 0, 512)])
-    dma("s", T.ein[:, 4 * H:4 * S], T.e[:, 4 * H:4 * S], [], [v("ein", 4 * H, 4 * S)])
+    def load_x(e, t):
+        dma(e, T.xin[:, 4 * W * t:4 * W * t + 512], T.x[:, 512 * t:512 * t + 512], [], [v("xin", 4 * W * t, 4 * W * t + 512)])
+    load_x("s", 0)
+    dma("a", T.ein[:, 0:4 * H1], T.e[:, 0:4 * H1], [], [v("ein", 0, 4 * H1)])
+    dma("s", T.ein[:, 4 * H1:4 * S], T.e[:, 4 * H1:4 * S], [], [v("ein", 4 * H1, 4 * S)])
     dma("a", T.pai[:], T.pa[:], [], [v("pai")])
-    dma("a", T.pbi[:], T.pb[:], [], [v("pbi")])
-    for t in (1, 2, 3):
-        dma("a" if t == 2 else "s", T.xin[:, 4 * W * t:4 * W * t + 512], T.x[:, 512 * t:512 * t + 512], [],
-            [v("xin", 4 * W * t, 4 * W * t + 512)])
+    dma("s", T.pbi[:], T.pb[:], [], [v("pbi")])
+    load_x("a", 1)
+    load_x("s", 2)
+    load_x("a", 3)
+    dma("s", T.vin[:], T.v[:], [], [v("vin")])
 
     iota(v("pci"), [[0, 1]], 0, 1, True)
     iota(v("jm16"), [[0, 8], [1, 16]], 0)
-    iota(v("trow"), [[-32, 4]], 111)
+    iota(v("ab", 0, 4), [[0, 2], [1, 2]], 0)
+    iota(v("ab", 4, 8), [[1, 2], [0, 2]], 0)
+    iota(v("trow"), [[16, 2], [-32, 4]], 111)
     iota(v("kmin"), [[-W, 4], [0, 2], [30000, 16]], 3 * W)
     iota(v("gz"), [[0, 512]], 0)
     iota(v("i448"), [[1, S]], 0)
@@ -302,50 +321,61 @@ def rank_program(g, core, T, topo):
     iota(v("t16"), [[CAP, 4]], 0)
     iota(v("cb", 0, 6), [[S, 2], [0, 3]], 0)
     iota(v("cb", 6, 12), [[S, 2], [2 * S, 3]], 2 * S)
-    iota(v("tli"), [[-1, 4], [0, 2]], 3, 0, True)
     iota(v("j16"), [[16, 8]], 128)
     iota(v("valrow"), [[PC, 8], [1, 16]], HW)
     iota(v("inv", 128, 256), [[0, 128]], 0)
     iota(v("rl", 0, 40), [[0, 40]], 128)
-    dma("g", T.vin[:], T.v[:], [], [v("vin")])
 
     for t in range(TT):
         memset(v("xin", 4 * W * t + 512, 4 * W * (t + 1)), 0.0)
-    for q in range(4):
-        for a in range(4):
-            memset(v("xa", a, a + 1, 1, 32 * q, 32 * q + 32), float(128 * ((q ^ a) >> 1) + 256 * ((q ^ a) & 1)))
     ts(v("bitsi", 0, 1), v("pci"), 15, None, ALU.bitwise_and)
-    ts(v("bitsi", 1, 2), v("pci"), 4, 1, ALU.logical_shift_right, ALU.bitwise_and)
-    cp(v("bits", 0, 2), v("bitsi"))
-    for pos in range(N):
-        ts(v("ft", 4 * pos, 4 * pos + 4), v("trow"), v("xa", order[pos] >> 1, (order[pos] >> 1) + 1), float(16 * (order[pos] & 1)),
-           ALU.add, ALU.add)
+    for j in (1, 2, 3):
+        ts(v("bitsi", j, j + 1), v("pci"), 3 + j, 1, ALU.logical_shift_right, ALU.bitwise_and)
+    cp(v("bits", 0, 4), v("bitsi"))
+    for j in (0, 1):
+        ts(v("xa", 4 + 4 * j, 8 + 4 * j), v("ab", 4 * j, 4 * j + 4), v("bits", 2 + j, 3 + j), float(256 >> j), ALU.not_equal, ALU.mult)
     ts(v("mask"), v("jm16"), icol, None, ALU.is_equal)
+    tt(v("xa", 0, 4), v("xa", 4, 8), v("xa", 8, 12), ALU.add)
+    for pos in range(N):
+        a, e = order[pos] >> 1, order[pos] & 1
+        o, i, b = v("ft", 4 * pos, 4 * pos + 4), v("trow", 4 * e, 4 * e + 4), v("xa", a, a + 1)
+        do("a", lambda: g.scalar.activation(o["ap"], i["ap"], ACT.Identity, bias=b["ap"]), [i, b], [o])
     ts(v("rst"), v("jm16"), 0.5, None, ALU.is_ge)
     ts(capcol, icol, 1.0, None, ALU.add)
-    tt(v("ft2"), v("ft"), v("mask", 0, 32), ALU.mult)
     ts(v("cap"), v("mask"), 0.0, capcol, ALU.mult, ALU.add)
+    cp(v("maskb"), v("mask"))
+    tt(v("ft2"), v("ft"), v("mask", 0, 32), ALU.mult)
     scan(v("ft3"), v("rst", 0, 32), v("ft2"), 0.0, ALU.mult, ALU.add)
     cp(v("fl"), v("ft3", 15, 32, 16))
-    quant("qe", 0, H, "ein", 0)
 
     def decode(x, stride, prep, first=None, late=None):
+        ahead = 0 if first else 1
+        h = H1 if first else H
         prep(0)
-        mm(0, x, 0, "qe", 0, H)
         if first:
-            first()
-        mm(1, x, 0, "qe", H, H)
-        prep(1)
-        mm(2, x, stride, "qe", 0, S)
-        cp(v("aa", 0, H), v("ps0", 0, H))
-        acopy(v("aa", H, S), v("ps1", 0, H))
+            quant("qe", 0, h, "ein", 0)
+        mm(0, x, 0, "qe", 0, h)
+        if first:
+            quant("qe", h, S, "ein", h)
+        mm(1, x, 0, "qe", h, S - h)
+        if ahead:
+            prep(1)
+            mm(2, x, stride, "qe", 0, S)
+        if first:
+            acopy(v("aa", 0, h), v("ps0", 0, h))
+            cp(v("pau"), v("pai"))
+            cp(v("aa", h, S), v("ps1", 0, S - h))
+            cp(v("pbu"), v("pbi"))
+        else:
+            cp(v("aa", 0, h), v("ps0", 0, h))
+            acopy(v("aa", h, S), v("ps1", 0, S - h))
         for t in (1, 2, 3):
             prev = v("aa", S * (t - 1), S * t)
             for a, b in (B1, B2, B3):
                 acopy(v("bt", 2 * S * t + a, 2 * S * t + b), prev, v("pau", a // 16, b // 16))
-            if t < 3:
-                prep(t + 1)
-                mm(t + 2, x, stride * (t + 1), "qe", 0, S)
+            if t + ahead <= 3:
+                prep(t + ahead)
+                mm(t + ahead + 1, x, stride * (t + ahead), "qe", 0, S)
             elif late:
                 late()
 
@@ -366,13 +396,13 @@ def rank_program(g, core, T, topo):
 
     top = v("rr", S - 1, S)
 
-    def trace(at):
+    def trace(keep):
         sa, sb, lt = v("dcol", 2, 3), v("dcol", 3, 4), v("lt")
         below(sa, v("rr", 0, S - 160), top, S - 160)
         ts(lt, v("rr", S - 160, S), top, None, ALU.is_lt)
-        do("v", lambda: g.vector.tensor_reduce(sb["ap"], lt["ap"], AxisListType.X, ALU.add), [lt], [sb])
+        reduce(sb, lt, ALU.add)
         ts(v("bo", 8, 12), v("cb", 2, 12, 3), sa, sb, ALU.add, ALU.add)
-        ts(v("path", at + 3, at + 4), sa, sb, None, ALU.add)
+        keep(3, sa, sb)
         for t in (3, 2, 1):
             tt(v("gg"), v("bt"), v("mask", 0, 64), ALU.mult, v("bo", 4 * (t - 1), 4 * t))
             scan(v("sc"), v("rst", 0, 64), v("gg"), 0.0, ALU.mult, ALU.add)
@@ -380,11 +410,11 @@ def rank_program(g, core, T, topo):
             ts(d, v("sc", 63, 64), v("sc", 47, 48), v("sc", 31, 32), ALU.is_gt, ALU.mult)
             if t > 1:
                 ts(v("bo", 4 * (t - 2), 4 * (t - 1)), v("cb", t - 2, 12, 3), d, v("sc", 15, 16), ALU.add, ALU.add)
-            ts(v("path", at + t - 1, at + t), d, v("sc", 15, 16), None, ALU.add)
+            keep(t - 1, d, v("sc", 15, 16))
 
-    def spread(at, d0, init, op0):
-        transpose(v("tr"), v("mi"))
-        scan(v("gz", 0, 128), d0, v("tr"), init, op0, ALU.add)
+    def spread(at, mi, tr, d0, init, op0, op1):
+        transpose(v(tr), v(mi))
+        scan(v("gz", 0, 128), d0, v(tr), init, op0, op1)
         cp(v("gz", 143, 256, 16, 64, 128), v("gz", 15, 128, 16, 0, 64))
         cp(v("gz", 143, 256, 16, 0, 64), v("gz", 15, 128, 16, 64, 128))
         for q in (3, 2, 1, 0):
@@ -402,8 +432,8 @@ def rank_program(g, core, T, topo):
                ALU.subtract, ALU.is_equal)
         scan(v("cum"), v("eq"), v("cap"), 0.0, ALU.add, ALU.min)
         below(v("dcol", 1, 2), v("cum"), capcol, 128)
-        ts(v("mi"), v("mask"), v("dcol", 1, 2), None, ALU.mult)
-        spread(at, v("kmin"), 1.0e9, ALU.min)
+        ts(v("mib"), v("maskb"), v("dcol", 1, 2), None, ALU.mult)
+        spread(at, "mib", "trb", v("kmin"), 1.0e9, ALU.min, ALU.add)
 
     def homelist(at, base, stride):
         w = [v("w8", 8 * k, 8 * k + 8) for k in range(8)]
@@ -432,11 +462,7 @@ def rank_program(g, core, T, topo):
         held, win, out, land, xs, ep, new, nt = ["%s%d" % (n, turn) for n in ("held", "win", "out", "land", "xs", "ep", "new", "nt")]
         k = 2 * turn - 1
         if turn == 1:
-            def first():
-                quant("qe", H, S, "ein", H)
-                cp(v("pau"), v("pai"))
-                cp(v("pbu"), v("pbi"))
-            decode(held, W, lambda t: quant("held1", W * t, W * (t + 1), "xin", W * t), first)
+            decode(held, W, lambda t: quant("held1", W * t, W * (t + 1), "xin", W * t), True)
         else:
             decode(held, W, lambda t: pick("held2", W * t, W * (t + 1), "win1", HW + 512, v("rlu", 10 * t, 10 * t + 9)))
         for f in (0, 1):
@@ -444,7 +470,7 @@ def rank_program(g, core, T, topo):
             dma("s", side(T, win, f, 0, HW), side(T, held, f, 0, HW), [v(held + x)], [v(win + x, 0, HW)])
         fo = 64 * (turn - 1)
         slots(fo)
-        for a, b in ((0, CH), (CH, CD), (CD, CS)):
+        for a, b in PICKS[turn]:
             pick(out, a, b, held, HW, v("offs", fo + a // 16, fo + b // 16))
         sends(k)
         pick(land, CS, 512, held, HW, v("offs", fo + CS // 16, fo + 32))
@@ -457,36 +483,33 @@ def rank_program(g, core, T, topo):
                 ts(v("et", 512 * b + b, 512 * (b + 1), 4), v("i448", 0, 128), v("pcf"), None, ALU.is_equal)
             tt(v("bt", S, 2 * S), v("i448"), v("bt", 0, S), ALU.subtract, v("pbu"))
             quant("qk", 0, 512, "et", 0)
-            cp(v("tl"), v("tli"))
+            ts(v("off32"), v("mask", 0, 32), 1.0, 4096.0, ALU.subtract, ALU.mult)
+            ts(v("cut"), v("rst"), 1.0, 4096.0, ALU.subtract, ALU.mult)
             ts(v("j128"), v("j16"), icol, None, ALU.add)
             ts(v("ownl"), v("t16"), icol, float(CS), ALU.add, ALU.add)
-            quant("qv", 0, 128, "vin", 0)
             homelist(fo, 0, 10)
         else:
-            trace(0)
-            homelist(fo, 40, 8)
+            trace(lambda t, x, y: ts(v("path", t, t + 1), x, y, None, ALU.add))
         arrivals(k)
         if turn == 2:
             dma("s", T.ol[:], T.path[:, 0:4], [v("path", 0, 4), v(land + "s")], [])
 
         def held_part(part):
             a, b, banks = part
-            for j in range(4):
+            for j in (0, 2, 1, 3):
                 mm(banks[j], "qk", 128 * j, land, a, b - a, True, False)
         decode(xs, 128, lambda t: pick(xs, 128 * t, 128 * (t + 1), land, 512, v("xl", 8 * t, 8 * t + 8)),
                None, lambda: held_part(parts[0]))
         held_part(parts[1])
-        at = 8 * turn
-        trace(at)
-        tt(v("mi"), v("path", at, at + 4), v("mask"), ALU.mult, v("tl"))
-        if turn == 2:
-            dma("s", T.dl[:], T.path[:, at:at + 4], [v("path", at, at + 4)], [])
-        spread(fo + 32, v("rst"), 0.0, ALU.mult)
+        at = 8
+        trace(lambda t, x, y: ts(v("mi", 96 - 32 * t, 128 - 32 * t), v("off32"), x, y, ALU.add, ALU.add))
+        spread(fo + 32, "mi", "tr", v("cut"), 0.0, ALU.add, ALU.max)
         for a, b, banks in parts:
             pick(ep, a, b, "qe", S, v("offs", fo + 32 + a // 16, fo + 32 + b // 16))
-            for j in range(4):
+            for j in (0, 2, 1, 3):
                 mm(banks[j], "qk", 128 * j, ep, a, b - a, False, True)
-        for a, b, part in ((0, CH, parts[0]), (CH, CD, parts[1]), (CD, 512, parts[1])):
+        for a, b in SUBS:
+            part = parts[int(a >= CH)]
             for j in (0, 2, 1, 3):
                 o, i = v(nt, 4 * a + j, 4 * b, 4), v("ps%d" % part[2][j], a - part[0], b - part[0])
                 if j < 2:
@@ -496,19 +519,27 @@ def rank_program(g, core, T, topo):
             quant(new, a, b, nt, a)
         sends(k + 1)
         pick(win, HW + CS, HW + 512, new, 512, v("ownl"))
+        if turn == 1:
+            quant("qv", 0, 128, "vin", 0)
+        else:
+            for t in range(TT):
+                reduce(v("path", at + t, at + t + 1), v("mi", 96 - 32 * t, 128 - 32 * t), ALU.max)
+            homelist(fo, 40, 8)
         arrivals(k + 1)
+        if turn == 2:
+            dma("s", T.dl[:], T.path[:, at:at + 4], [v("path", at, at + 4), v(win + "c", HW, HW + CS)], [])
 
     for j in (0, 1):
         a, b = 256 * j, 256 * (j + 1)
         pick("fin", a, b, "win2", HW + 512, v("rlu", 40 + 16 * j, 56 + 16 * j))
         mm(5 + j, "qv", 0, "fin", a, 256)
         dma("s", T.oc[:, 4 * a:4 * b], side(T, "fin", 0, a, b), [v("finc", a, b)], [])
+    for q in range(4):
+        dma("s" if q < 2 else "a", T.osc[4 * q:4 * q + 4, :], T.fins[32 * q:32 * q + 4, :], [v("fins", 0, 512, 1, 32 * q, 32 * q + 4)], [])
     cp(v("ysb", 0, 256), v("ps5", 0, 256))
     dma("s", T.y[:, 0:256], T.ysb[:, 0:256], [v("ysb", 0, 256)], [])
     acopy(v("ysb", 256, 512), v("ps6", 0, 256))
     dma("a", T.y[:, 256:512], T.ysb[:, 256:512], [v("ysb", 256, 512)], [])
-    for q in range(4):
-        dma("s" if q < 2 else "a", T.osc[4 * q:4 * q + 4, :], T.fins[32 * q:32 * q + 4, :], [v("fins", 0, 512, 1, 32 * q, 32 * q + 4)], [])
 
     count["sent"] = sent[0]
     for sem in count:

from concourse.bass import DstId, RemoteDMATransfer
from concourse.mybir import dt, AluOpType, ActivationFunctionType, AxisListType

ALU = AluOpType
ACT = ActivationFunctionType
N, TT, S, CAP = 8, 4, 448, 16
W = 144
HW = TT * W
PC = TT * CAP
NH = 4
B1, B2, B3 = (0, 128), (128, 288), (288, S)
C4, U8 = "float8_e4m3fn_x4", "uint8"
CS = PC * (N - 1)
PICKS = {1: ((128, 384), (0, 128), (384, CS)), 2: ((0, 256), (256, CS))}
CH = 256
SUBS = ((0, 256), (256, 512))

SCRATCH = {}
for _d, _l in (("bfloat16", "xin 2304 ein 1792 vin 512 et 2048 nt1 2048 nt2 2048 cap 128 db 32 row 128 eq 128 cum 128 "
                            "maskb 128 mib 128 trb 128"),
               ("int32", "pai 28 pbi 28 pci 1 bitsi 4"),
               ("uint16", "pau 28 pbu 28 fl 2 offs 128 xl 32 ro 8 rlu 80 bo 12 ownl 4"),
               ("float32", "aa 1792 bt 3584 rr 448 junk 448 lt 160 ysb 512 pcf 1 bits 5 jm16 128 mask 128 rst 128 kmin 128 i448 448 "
                           "trow 8 ab 8 xa 12 ft 32 ft2 32 ft3 32 gz 512 mi 128 tr 128 dcol 4 t16 4 cb 12 j16 8 j128 8 valrow 128 "
                           "inv 256 w8 64 rl 80 gg 64 sc 64 dd 4 path 24 off32 32 cut 128")):
    _l = _l.split()
    for _k in range(0, len(_l), 2):
        SCRATCH[_l[_k]] = ("sbuf", [128, int(_l[_k + 1])], _d)
for _n, _w in (("qe", S), ("qv", 128), ("qk", 512), ("held1", HW), ("held2", HW), ("win1", HW + 512), ("win2", HW + 512),
               ("out1", 512), ("out2", 512), ("land1", 512), ("land2", 512), ("xs1", 512), ("xs2", 512), ("ep1", 512), ("ep2", 512),
               ("new1", 512), ("new2", 512), ("fin", 512), ("rel1", PC * NH), ("rel2", PC * NH), ("rel3", PC * NH), ("rel4", PC * NH)):
    SCRATCH[_n + "c"] = ("sbuf", [128, _w], C4)
    SCRATCH[_n + "s"] = ("sbuf", [128, _w], U8)
for _b in range(8):
    SCRATCH["ps%d" % _b] = ("psum", [128, 512], "float32")

SEMAPHORES = (["cv", "ca", "cp", "cg", "sent"] + ["%s%d" % (a, k) for a in ("arrc", "arrs", "rel0", "rel1") for k in range(1, 5)]
              + ["d%d" % k for k in range(40)])

STAGES = {1: ("out1", "land1", 0), 2: ("new1", "win1", HW), 3: ("out2", "land2", 0), 4: ("new2", "win2", HW)}


def bits_of(engs):
    m = 0
    for e in engs:
        m |= 1 << e
    return m


def deal(n, engs):
    s = len(engs) // n
    return [engs[s * k:s * (k + 1)] for k in range(n)]


def routes(cores, topo):
    def on_chip(ch):
        return [k for k in range(N) if topo.chip(cores[k]) == ch]

    def far_chips(ch):
        return sorted({topo.chip(c) for c in cores if topo.chip(c) != ch and not topo.same_plane(ch, topo.chip(c))})

    def helpers(r):
        c = cores[r]
        far = cores[on_chip(far_chips(topo.chip(c))[0])[0]]
        free = [k for k in topo.cores_of(c) if k not in cores]
        hx = [k for k in free if topo.may_write(k, far)]
        hp = [k for k in free if k not in hx and topo.die(k) != topo.die(c)]
        hq = [k for k in free if k not in hx and k not in hp]
        place = on_chip(topo.chip(c)).index(r)
        return hx[place], hp[place], hq[place]

    plan = []
    for r, c in enumerate(cores):
        ch = topo.chip(c)
        here = on_chip(ch)
        near = [k for k in range(N) if topo.same_plane(ch, topo.chip(cores[k]))]
        far = far_chips(ch)
        y1, y2 = far[here.index(r)], far[1 - here.index(r)]
        hx, hp, hq = helpers(r)
        order = near + on_chip(y1) + on_chip(y2) + [k for k in here if k != r] + [r]
        lo = topo.engines(c, cores[near[0]])
        hi = [e for e in topo.engines(c, hq) if e not in lo]

        def direct(a, engs, n=2):
            return [(a + j, 1, None, m, 0) for j, m in enumerate(deal(n, engs))]
        out = [(0, [(0, 2, hp, hi, 0), (2, 2, hx, lo, 0)]), (1, [(0, 2, hq, hi, 0)]),
               (0, direct(4, lo) + direct(6, hi, 1)), (1, direct(2, lo, 4) + direct(6, hi, 1))]
        half = deal(2, hi)
        first = [(0, direct(2, lo, 4)), (0, [(0, 2, hp, hi, 0)]), (1, [(0, 2, hq, half[0], 0), (2, 2, hx, half[1], 0)]),
                 (1, direct(4, lo) + direct(6, hi, 1)), (0, direct(6, hi, 1))]
        ways = []
        for calls in (first, out, out, out):
            eng, relay = {}, []
            for f, trs in calls:
                for a, n, to, e, slot in trs:
                    if to is None:
                        eng[order[a], f] = e
                    else:
                        relay.append((slot, to, f, a, n, len(e)))
                        for j, m in enumerate(deal(n, topo.engines(to, cores[order[a]]))):
                            eng[order[a + j], f] = m
            ways.append({"calls": calls, "relay": relay, "eng": eng})
        plan.append({"order": order, "ways": ways})
    return plan


def side(T, name, f, a, b):
    return T[name + "s"][:, a:b] if f else T[name + "c"][:, a:b].bitcast(dt.uint8)


def landing(T, plan, r, d, k, f):
    _, land, base = STAGES[k]
    c = base + PC * plan[d]["order"].index(r)
    return side(T, land, f, c, c + PC), T.sem[("arrs%d" if f else "arrc%d") % k]


def transfer(topo, core, engs, src, dst, sem):
    rid, pid, _ = topo.addr(core)
    return RemoteDMATransfer(dst_ids=[DstId(rid=rid, pnc=pid)], dma_engine_mask=bits_of(engs), remote_sem=sem, src=src, dst=dst)


def helper_program(g, T, topo, plan, core):
    sent = 0
    for k in range(1, 5):
        for (slot, _, f, a, n, count), r in sorted((j, r) for r in range(N) for j in plan[r]["ways"][k - 1]["relay"] if j[1] == core):
            eng = plan[r]["ways"][k - 1]["eng"]
            g.wait_ge(T.sem["rel%d%d" % (slot, k)], count)
            trs = []
            for j in range(n):
                d = plan[r]["order"][a + j]
                dst, sem = landing(T, plan, r, d, k, f)
                at = PC * (2 * slot + j)
                trs.append(transfer(topo, T.cores[d], eng[d, f], side(T, "rel%d" % k, f, at, at + PC), dst, sem))
                sent += len(eng[d, f])
            g.remote_dma_fused(trs, local_sem=T.sem.sent)
    if sent:
        g.wait_ge(T.sem.sent, sent)


def rank_program(g, core, T, topo):
    plan = routes(list(T.cores), topo)
    r = T.rank_of(core)
    if r is None:
        helper_program(g, T, topo, plan, core)
        return
    me = plan[r]
    order = me["order"]
    Q = {"v": g.vector, "a": g.scalar, "p": g.tensor, "s": g.sync, "g": g}
    known = {e: {} for e in Q}
    count, waited, hist = {}, {}, {}
    seq, free = [0], ["d%d" % k for k in range(40)]

    def v(name, a=0, b=None, step=1, p0=0, p1=128):
        if b is None:
            b = SCRATCH[name][1][1]
        m = 0
        if step == 1:
            m = ((1 << (b - a)) - 1) << a
        else:
            for c in range(a, b, step):
                m |= 1 << c
        cs = slice(a, b) if step == 1 else slice(a, b, step)
        ap = T[name][:, cs] if (p0, p1) == (0, 128) else T[name][p0:p1, cs]
        return {"ap": ap, "n": name, "p": (p0, p1), "m": m}

    def wait(e, sem, n, clock):
        if known[e].get(sem, 0) >= n:
            return
        Q[e].wait_ge(T.sem[sem], n)
        waited[sem] = max(waited.get(sem, 0), n)
        known[e][sem] = n
        for s, c in clock.items():
            if known[e].get(s, 0) < c:
                known[e][s] = c

    def before(e, reads, writes):
        deps = {}
        for views, wr in ((reads, False), (writes, True)):
            for x in views:
                for (op, w, p, m) in hist.get(x["n"], []):
                    if x["n"].startswith("ps"):
                        hit = op["e"] != e
                    else:
                        hit = (w or wr) and p[0] < x["p"][1] and x["p"][0] < p[1] and (m & x["m"])
                    if hit:
                        deps[op["k"]] = op
        for k in sorted(deps, reverse=True):
            wait(e, deps[k]["sem"], deps[k]["n"], deps[k]["clock"])

    def note(e, sem, n, reads, writes, clock):
        seq[0] += 1
        op = {"e": e, "sem": sem, "n": n, "k": seq[0], "clock": clock}
        for views, wr in ((reads, False), (writes, True)):
            for x in views:
                hist.setdefault(x["n"], []).append((op, wr, x["p"], x["m"]))

    def do(e, call, reads, writes):
        before(e, reads, writes)
        sem = "c" + e
        count[sem] = count.get(sem, 0) + 1
        call().then_inc(T.sem[sem], 1)
        note(e, sem, count[sem], reads, writes, dict(known[e]))

    def dma(e, out, in_, reads, writes):
        before(e, reads, writes)
        sem = free.pop(0)
        count[sem] = 16
        Q[e].dma_start(out, in_).then_inc(T.sem[sem], 16)
        note("d", sem, 16, reads, writes, dict(known[e]))

    def sc(x):
        return x["ap"] if isinstance(x, dict) else x

    def cols(*xs):
        return [x for x in xs if isinstance(x, dict)]

    def src(x, off):
        return x["ap"] if off is None else x["ap"].indirect(off["ap"])

    def ts(out, in0, s1, s2, op0, op1=None):
        if op1 is None:
            do("v", lambda: g.vector.tensor_scalar(out["ap"], in0["ap"], sc(s1), None, op0), cols(in0, s1), [out])
        else:
            do("v", lambda: g.vector.tensor_scalar(out["ap"], in0["ap"], sc(s1), sc(s2), op0, op1), cols(in0, s1, s2), [out])

    def tt(out, in0, in1, op, off=None):
        do("v", lambda: g.vector.tensor_tensor(out["ap"], src(in0, off), in1["ap"], op), cols(in0, in1, off), [out])

    def cp(out, in_, off=None):
        do("v", lambda: g.vector.tensor_copy(out["ap"], src(in_, off)), cols(in_, off), [out])

    def scan(out, d0, d1, init, op0, op1):
        do("v", lambda: g.vector.tensor_tensor_scan(out["ap"], d0["ap"], d1["ap"], init, op0, op1), [d0, d1], [out])

    def reduce(out, in_, op):
        do("v", lambda: g.vector.tensor_reduce(out["ap"], in_["ap"], AxisListType.X, op), [in_], [out])

    def transpose(out, in_):
        do("v", lambda: g.vector.transpose(out["ap"], in_["ap"]), [in_], [out])

    def memset(out, c):
        do("v", lambda: g.vector.memset(out["ap"], c), [], [out])

    def acopy(out, in_, off=None):
        do("a", lambda: g.scalar.activation(out["ap"], src(in_, off), ACT.Copy), cols(in_, off), [out])

    def below(acc, in_, top, n):
        j = v("junk", 0, n)
        do("a", lambda: g.scalar.activation(j["ap"], in_["ap"], ACT.Sign, bias=top["ap"], scale=-1.0, accum_out=acc["ap"]),
           [in_, top], [j, acc])

    def iota(out, pattern, base, cm=0, whole=False):
        if whole:
            do("g", lambda: g.iota(out["ap"], pattern, base, cm), [], [out])
        else:
            do("g", lambda: g.iota(out["ap"], pattern, base, cm, allow_small_or_imprecise_dtypes=True), [], [out])

    def quant(name, a, b, tile, ta):
        c, s, t = v(name + "c", a, b), v(name + "s", a, b), v(tile, 4 * ta, 4 * (ta + b - a))
        do("v", lambda: g.vector.quantize_mx(c["ap"], s["ap"], t["ap"]), [t], [c, s])

    def pick(dst, a, b, win, n, off):
        o, w = v(dst + "c", a, b), v(win + "c", 0, n)
        do("v", lambda: g.vector.tensor_copy(o["ap"].bitcast(dt.uint32), w["ap"].bitcast(dt.uint32).indirect(off["ap"])), [w, off], [o])
        acopy(v(dst + "s", a, b), v(win + "s", 0, n), off)

    def mm(bank, w, wa, x, xa, n, start=True, stop=True):
        o = v("ps%d" % bank, 0, n)
        wc, ws, xc, xs = v(w + "c", wa, wa + 128), v(w + "s", wa, wa + 128), v(x + "c", xa, xa + n), v(x + "s", xa, xa + n)
        do("p", lambda: g.tensor.matmul_mx(o["ap"], wc["ap"], ws["ap"], xc["ap"], xs["ap"], start, stop), [wc, ws, xc, xs], [o])

    sent = [0]

    def sends(k):
        name = STAGES[k][0]
        for f, trs in me["ways"][k - 1]["calls"]:
            x = "s" if f else "c"
            before("g", [v(name + x, PC * a, PC * (a + n)) for a, n, to, e, slot in trs], [])
            out = []
            for a, n, to, e, slot in trs:
                if to is None:
                    dst, sem = landing(T, plan, r, order[a], k, f)
                    to = T.cores[order[a]]
                else:
                    dst, sem = side(T, "rel%d" % k, f, 2 * PC * slot, PC * (2 * slot + n)), T.sem["rel%d%d" % (slot, k)]
                out.append(transfer(topo, to, e, side(T, name, f, PC * a, PC * (a + n)), dst, sem))
                sent[0] += len(e)
            g.remote_dma_fused(out, local_sem=T.sem.sent)

    def arrivals(k):
        _, land, base = STAGES[k]
        for f in (0, 1):
            sem = ("arrs%d" if f else "arrc%d") % k
            count[sem] = sum(len(plan[h]["ways"][k - 1]["eng"][r, f]) for h in range(N) if h != r)
            note("r", sem, count[sem], [], [v(land + ("s" if f else "c"), base, base + CS)], {})

    icol, capcol = v("bits", 0, 1), v("bits", 4, 5)
    H, H1 = S // 2, 320

    def load_x(e, t):
        dma(e, T.xin[:, 4 * W * t:4 * W * t + 512], T.x[:, 512 * t:512 * t + 512], [], [v("xin", 4 * W * t, 4 * W * t + 512)])
    load_x("s", 0)
    dma("a", T.ein[:, 0:4 * H1], T.e[:, 0:4 * H1], [], [v("ein", 0, 4 * H1)])
    dma("s", T.ein[:, 4 * H1:4 * S], T.e[:, 4 * H1:4 * S], [], [v("ein", 4 * H1, 4 * S)])
    dma("a", T.pai[:], T.pa[:], [], [v("pai")])
    dma("s", T.pbi[:], T.pb[:], [], [v("pbi")])
    load_x("a", 1)
    load_x("s", 2)
    load_x("a", 3)
    dma("s", T.vin[:], T.v[:], [], [v("vin")])

    iota(v("pci"), [[0, 1]], 0, 1, True)
    iota(v("jm16"), [[0, 8], [1, 16]], 0)
    iota(v("ab", 0, 4), [[0, 2], [1, 2]], 0)
    iota(v("ab", 4, 8), [[1, 2], [0, 2]], 0)
    iota(v("trow"), [[16, 2], [-32, 4]], 111)
    iota(v("kmin"), [[-W, 4], [0, 2], [30000, 16]], 3 * W)
    iota(v("gz"), [[0, 512]], 0)
    iota(v("i448"), [[1, S]], 0)
    iota(v("pcf"), [[0, 1]], 0, 1)
    iota(v("t16"), [[CAP, 4]], 0)
    iota(v("cb", 0, 6), [[S, 2], [0, 3]], 0)
    iota(v("cb", 6, 12), [[S, 2], [2 * S, 3]], 2 * S)
    iota(v("j16"), [[16, 8]], 128)
    iota(v("valrow"), [[PC, 8], [1, 16]], HW)
    iota(v("inv", 128, 256), [[0, 128]], 0)
    iota(v("rl", 0, 40), [[0, 40]], 128)

    for t in range(TT):
        memset(v("xin", 4 * W * t + 512, 4 * W * (t + 1)), 0.0)
    ts(v("bitsi", 0, 1), v("pci"), 15, None, ALU.bitwise_and)
    for j in (1, 2, 3):
        ts(v("bitsi", j, j + 1), v("pci"), 3 + j, 1, ALU.logical_shift_right, ALU.bitwise_and)
    cp(v("bits", 0, 4), v("bitsi"))
    for j in (0, 1):
        ts(v("xa", 4 + 4 * j, 8 + 4 * j), v("ab", 4 * j, 4 * j + 4), v("bits", 2 + j, 3 + j), float(256 >> j), ALU.not_equal, ALU.mult)
    ts(v("mask"), v("jm16"), icol, None, ALU.is_equal)
    tt(v("xa", 0, 4), v("xa", 4, 8), v("xa", 8, 12), ALU.add)
    for pos in range(N):
        a, e = order[pos] >> 1, order[pos] & 1
        o, i, b = v("ft", 4 * pos, 4 * pos + 4), v("trow", 4 * e, 4 * e + 4), v("xa", a, a + 1)
        do("a", lambda: g.scalar.activation(o["ap"], i["ap"], ACT.Identity, bias=b["ap"]), [i, b], [o])
    ts(v("rst"), v("jm16"), 0.5, None, ALU.is_ge)
    ts(capcol, icol, 1.0, None, ALU.add)
    ts(v("cap"), v("mask"), 0.0, capcol, ALU.mult, ALU.add)
    cp(v("maskb"), v("mask"))
    tt(v("ft2"), v("ft"), v("mask", 0, 32), ALU.mult)
    scan(v("ft3"), v("rst", 0, 32), v("ft2"), 0.0, ALU.mult, ALU.add)
    cp(v("fl"), v("ft3", 15, 32, 16))

    def decode(x, stride, prep, first=None, late=None):
        ahead = 0 if first else 1
        h = H1 if first else H
        prep(0)
        if first:
            quant("qe", 0, h, "ein", 0)
        mm(0, x, 0, "qe", 0, h)
        if first:
            quant("qe", h, S, "ein", h)
        mm(1, x, 0, "qe", h, S - h)
        if ahead:
            prep(1)
            mm(2, x, stride, "qe", 0, S)
        if first:
            acopy(v("aa", 0, h), v("ps0", 0, h))
            cp(v("pau"), v("pai"))
            cp(v("aa", h, S), v("ps1", 0, S - h))
            cp(v("pbu"), v("pbi"))
        else:
            cp(v("aa", 0, h), v("ps0", 0, h))
            acopy(v("aa", h, S), v("ps1", 0, S - h))
        for t in (1, 2, 3):
            prev = v("aa", S * (t - 1), S * t)
            for a, b in (B1, B2, B3):
                acopy(v("bt", 2 * S * t + a, 2 * S * t + b), prev, v("pau", a // 16, b // 16))
            if t + ahead <= 3:
                prep(t + ahead)
                mm(t + ahead + 1, x, stride * (t + ahead), "qe", 0, S)
            elif late:
                late()

            def larger(a, b):
                tt(v("bt", 2 * S * t + S + a, 2 * S * t + S + b), prev, v("bt", 2 * S * t + a, 2 * S * t + b), ALU.max,
                   v("pbu", a // 16, b // 16))

            def add(a, b):
                tt(v("aa", S * t + a, S * t + b), v("bt", 2 * S * t + S + a, 2 * S * t + S + b), v("ps%d" % (t + 1), a, b), ALU.add)
            larger(*B1)
            larger(*B2)
            add(*B1)
            larger(*B3)
            add(*B2)
            add(*B3)
        last = v("aa", 3 * S, 4 * S)
        scan(v("rr"), last, last, -1.0e29, ALU.max, ALU.max)

    top = v("rr", S - 1, S)

    def trace(keep):
        sa, sb, lt = v("dcol", 2, 3), v("dcol", 3, 4), v("lt")
        below(sa, v("rr", 0, S - 160), top, S - 160)
        ts(lt, v("rr", S - 160, S), top, None, ALU.is_lt)
        reduce(sb, lt, ALU.add)
        ts(v("bo", 8, 12), v("cb", 2, 12, 3), sa, sb, ALU.add, ALU.add)
        keep(3, sa, sb)
        for t in (3, 2, 1):
            tt(v("gg"), v("bt"), v("mask", 0, 64), ALU.mult, v("bo", 4 * (t - 1), 4 * t))
            scan(v("sc"), v("rst", 0, 64), v("gg"), 0.0, ALU.mult, ALU.add)
            d = v("dd", t, t + 1)
            ts(d, v("sc", 63, 64), v("sc", 47, 48), v("sc", 31, 32), ALU.is_gt, ALU.mult)
            if t > 1:
                ts(v("bo", 4 * (t - 2), 4 * (t - 1)), v("cb", t - 2, 12, 3), d, v("sc", 15, 16), ALU.add, ALU.add)
            keep(t - 1, d, v("sc", 15, 16))

    def spread(at, mi, tr, d0, init, op0, op1):
        transpose(v(tr), v(mi))
        scan(v("gz", 0, 128), d0, v(tr), init, op0, op1)
        cp(v("gz", 143, 256, 16, 64, 128), v("gz", 15, 128, 16, 0, 64))
        cp(v("gz", 143, 256, 16, 0, 64), v("gz", 15, 128, 16, 64, 128))
        for q in (3, 2, 1, 0):
            o = q ^ 1
            cp(v("gz", 271, 512, 16, 32 * q, 32 * q + 32), v("gz", 15, 256, 16, 32 * o, 32 * o + 32))
        cp(v("offs", at, at + 32), v("gz"), v("fl"))

    def slots(at):
        below(v("dcol", 0, 1), v("rr", S // N - 1, S, S // N), top, N)
        ts(v("db"), v("mask", 0, 32), 0.0, v("dcol", 0, 1), ALU.mult, ALU.add)
        for a in range(4):
            transpose(v("row", 32 * a, 32 * a + 32, 1, 0, 32), v("db", 0, 32, 1, 32 * a, 32 * a + 32))
        for q in range(4):
            ts(v("eq", 0, 128, 1, 32 * q, 32 * q + 32), v("row", 0, 128, 1, 0, 32), float(2 * q), v("bits", 1, 2, 1, 0, 32),
               ALU.subtract, ALU.is_equal)
        scan(v("cum"), v("eq"), v("cap"), 0.0, ALU.add, ALU.min)
        below(v("dcol", 1, 2), v("cum"), capcol, 128)
        ts(v("mib"), v("maskb"), v("dcol", 1, 2), None, ALU.mult)
        spread(at, "mib", "trb", v("kmin"), 1.0e9, ALU.min, ALU.add)

    def homelist(at, base, stride):
        w = [v("w8", 8 * k, 8 * k + 8) for k in range(8)]
        cp(w[0], v("offs", at, at + 32, 4))
        cp(v("inv", 0, 128), v("i448", 0, 128))
        ts(w[1], w[0], 128.0, None, ALU.is_ge)
        tt(w[2], w[1], v("j128"), ALU.mult)
        tt(w[3], w[2], w[0], ALU.max)
        cp(v("ro"), w[3])
        inv, ro, val = v("inv"), v("ro"), v("valrow")
        do("v", lambda: g.vector.tensor_copy(inv["ap"].indirect(ro["ap"]), val["ap"]), [ro, val], [inv])
        tt(v("mi"), v("inv", 0, 128), v("mask"), ALU.mult)
        scan(v("tr"), v("rst"), v("mi"), 0.0, ALU.mult, ALU.add)
        b8 = v("tr", 15, 128, 16)
        ts(w[4], b8, float(HW), float(CAP - W), ALU.is_ge, ALU.mult)
        cp(v("rl", base, base + 8), b8)
        for t in (1, 2, 3):
            ts(w[4 + t], w[4], float(W), float(t), ALU.add, ALU.mult)
        for t in (1, 2, 3):
            tt(v("rl", base + stride * t, base + stride * t + 8), w[4 + t], b8, ALU.add)
        cp(v("rlu", base, base + stride * TT), v("rl", base, base + stride * TT))

    parts = ((0, CH, (5, 6, 7, 1)), (CH, 512, (0, 2, 3, 4)))

    for turn in (1, 2):
        held, win, out, land, xs, ep, new, nt = ["%s%d" % (n, turn) for n in ("held", "win", "out", "land", "xs", "ep", "new", "nt")]
        k = 2 * turn - 1
        if turn == 1:
            decode(held, W, lambda t: quant("held1", W * t, W * (t + 1), "xin", W * t), True)
        else:
            decode(held, W, lambda t: pick("held2", W * t, W * (t + 1), "win1", HW + 512, v("rlu", 10 * t, 10 * t + 9)))
        for f in (0, 1):
            x = "s" if f else "c"
            dma("s", side(T, win, f, 0, HW), side(T, held, f, 0, HW), [v(held + x)], [v(win + x, 0, HW)])
        fo = 64 * (turn - 1)
        slots(fo)
        for a, b in PICKS[turn]:
            pick(out, a, b, held, HW, v("offs", fo + a // 16, fo + b // 16))
        sends(k)
        pick(land, CS, 512, held, HW, v("offs", fo + CS // 16, fo + 32))
        if turn == 1:
            for h in range(N):
                ts(v("xl", h, 32, 8), v("t16"), icol, float(PC * order.index(h)), ALU.add, ALU.add)
            acopy(v("bt", 0, S), v("i448"), v("pau"))
            memset(v("et"), 0.0)
            for b in range(4):
                ts(v("et", 512 * b + b, 512 * (b + 1), 4), v("i448", 0, 128), v("pcf"), None, ALU.is_equal)
            tt(v("bt", S, 2 * S), v("i448"), v("bt", 0, S), ALU.subtract, v("pbu"))
            quant("qk", 0, 512, "et", 0)
            ts(v("off32"), v("mask", 0, 32), 1.0, 4096.0, ALU.subtract, ALU.mult)
            ts(v("cut"), v("rst"), 1.0, 4096.0, ALU.subtract, ALU.mult)
            ts(v("j128"), v("j16"), icol, None, ALU.add)
            ts(v("ownl"), v("t16"), icol, float(CS), ALU.add, ALU.add)
            homelist(fo, 0, 10)
        else:
            trace(lambda t, x, y: ts(v("path", t, t + 1), x, y, None, ALU.add))
        arrivals(k)
        if turn == 2:
            dma("s", T.ol[:], T.path[:, 0:4], [v("path", 0, 4), v(land + "s")], [])

        def held_part(part):
            a, b, banks = part
            for j in (0, 2, 1, 3):
                mm(banks[j], "qk", 128 * j, land, a, b - a, True, False)
        decode(xs, 128, lambda t: pick(xs, 128 * t, 128 * (t + 1), land, 512, v("xl", 8 * t, 8 * t + 8)),
               None, lambda: held_part(parts[0]))
        held_part(parts[1])
        at = 8
        trace(lambda t, x, y: ts(v("mi", 96 - 32 * t, 128 - 32 * t), v("off32"), x, y, ALU.add, ALU.add))
        spread(fo + 32, "mi", "tr", v("cut"), 0.0, ALU.add, ALU.max)
        for a, b, banks in parts:
            pick(ep, a, b, "qe", S, v("offs", fo + 32 + a // 16, fo + 32 + b // 16))
            for j in (0, 2, 1, 3):
                mm(banks[j], "qk", 128 * j, ep, a, b - a, False, True)
        for a, b in SUBS:
            part = parts[int(a >= CH)]
            for j in (0, 2, 1, 3):
                o, i = v(nt, 4 * a + j, 4 * b, 4), v("ps%d" % part[2][j], a - part[0], b - part[0])
                if j < 2:
                    ts(o, i, 0.5, None, ALU.mult)
                else:
                    do("a", lambda: g.scalar.activation(o["ap"], i["ap"], ACT.Copy, scale=0.5), [i], [o])
            quant(new, a, b, nt, a)
        sends(k + 1)
        pick(win, HW + CS, HW + 512, new, 512, v("ownl"))
        if turn == 1:
            quant("qv", 0, 128, "vin", 0)
        else:
            for t in range(TT):
                reduce(v("path", at + t, at + t + 1), v("mi", 96 - 32 * t, 128 - 32 * t), ALU.max)
            homelist(fo, 40, 8)
        arrivals(k + 1)
        if turn == 2:
            dma("s", T.dl[:], T.path[:, at:at + 4], [v("path", at, at + 4), v(win + "c", HW, HW + CS)], [])

    for j in (0, 1):
        a, b = 256 * j, 256 * (j + 1)
        pick("fin", a, b, "win2", HW + 512, v("rlu", 40 + 16 * j, 56 + 16 * j))
        mm(5 + j, "qv", 0, "fin", a, 256)
        dma("s", T.oc[:, 4 * a:4 * b], side(T, "fin", 0, a, b), [v("finc", a, b)], [])
    for q in range(4):
        dma("s" if q < 2 else "a", T.osc[4 * q:4 * q + 4, :], T.fins[32 * q:32 * q + 4, :], [v("fins", 0, 512, 1, 32 * q, 32 * q + 4)], [])
    cp(v("ysb", 0, 256), v("ps5", 0, 256))
    dma("s", T.y[:, 0:256], T.ysb[:, 0:256], [v("ysb", 0, 256)], [])
    acopy(v("ysb", 256, 512), v("ps6", 0, 256))
    dma("a", T.y[:, 256:512], T.ysb[:, 256:512], [v("ysb", 256, 512)], [])

    count["sent"] = sent[0]
    for sem in count:
        if waited.get(sem, 0) < count[sem]:
            g.wait_ge(T.sem[sem], count[sem])
